import numpy as np, ml_dtypes
CORES = [6,15,38,47]
N = 4
BF = ml_dtypes.bfloat16
def gentries(a):
    return np.ascontiguousarray(a.reshape(8, 16, -1).transpose(0, 2, 1)).reshape(8, -1)
def gtable(e):
    e = np.asarray(e); return np.ascontiguousarray(e.reshape(8, -1, 16).transpose(0, 2, 1)).reshape(128, -1).astype(np.int32)
P, S, F, SW = 256, 8, 5, 2
V, RO = S * P, S - F
def node(rng, shape):
    return rng.integers(0, 2, shape) * V + rng.integers(0, F * P, shape)
def parts(rng):
    r = rng.integers(-1024, 1025, (N, 8, 16, F, P)); o = rng.integers(-256, 257, (N, 8, 16, S, P)); v = 0.5 + rng.random((N, 8, 16, S, P))
    m = rng.integers(0, 3, (N, 8, 16, 2 * (S - 1))); a = node(rng, (N, 8, F * P))
    return r, o, v, m, a
def lonely(rng, a):
    for q in range(N):
        for g in range(8):
            p = rng.permutation(P)[:7]
            for s in range(F):
                a[q, g, s * P + p[0]] = s * P + p[0]; a[q, g, s * P + p[1]] = s * P + p[2]; a[q, g, s * P + p[2]] = s * P + p[1]
                a[q, g, s * P + p[3]] = s * P + (p[4] if s else p[3]); a[q, g, s * P + p[4]] = s * P + p[3]
                a[q, g, s * P + p[5]] = s * P + (p[5] if s else p[6])
            a[q, g, p[6]] = p[5]
    return a
def pack(r, o, v, m, a):
    return {"r0": np.ascontiguousarray(r.reshape(N, 128, F * P)).astype(np.int32), "oc": o.reshape(N, 128, V).astype(np.float32).astype(BF), "stake": v.reshape(N, 128, V).astype(np.float32).astype(BF),
            "mu": m.reshape(N, 128, 2 * (S - 1)).astype(np.float32).astype(BF), "opp": np.stack([gtable(b) for b in a])}
def setup_inputs(rng):
    r, o, v, m, a = parts(rng)
    return pack(r, o, v, m, lonely(rng, a))
def setup_inputs_spread(rng):
    r, o, v, m, a = parts(rng)
    r = (np.exp2(4 + 6 * rng.random((N, 8, 1, F, P))) * (2 * rng.random(r.shape) - 1)).astype(np.int64)
    o = (np.exp2(8 * rng.random((N, 8, 1, S, P))) * (2 * rng.random(o.shape) - 1)).astype(np.int64)
    v = v * np.exp2(rng.integers(-1, 2, (N, 8, 1, S, P))); m = (3 * rng.random(m.shape) ** 2).astype(np.int64)
    a = rng.integers(0, 2, a.shape) * V + np.minimum((F * P * rng.random(a.shape) ** 2).astype(np.int64), F * P - 1)
    return pack(r, o, v, m, lonely(rng, a))
def setup_inputs_ends(rng):
    r, o, v, m, a = parts(rng); lo, hi = 0, V + F * P - 1
    r = np.where(rng.random(r.shape) < 0.5, -1024, 1024); o = np.where(rng.random(o.shape) < 0.5, -256, 256)
    v = np.where(rng.random(v.shape) < 0.5, 0.25, 4.0); m = 2 * rng.integers(0, 2, m.shape)
    a = np.where(rng.random(a.shape) < 0.7, np.where(rng.random(a.shape) < 0.5, lo, hi), a)
    b = np.where(rng.random((N, 8, P)) < 0.5, -1, 1); b[:, :, 0] = 1; b[:, :, P - 1] = -1
    for g in (0, 3, 5, 7):
        r[:, g] = 1024 * b[:, g, None, None, :]; o[:, g] = -256 * b[:, g, None, None, :]
        m[:, g, ::2] = 2; m[:, g, 15] = 2
        a[:, g] = np.where(rng.random((N, F * P)) < 0.8, np.tile(np.where(b[:, g] > 0, hi, lo), (1, F)), a[:, g])
    return pack(r, o, v, m, a)
def setup_inputs_corners(rng):
    r, o, v, m, a = parts(rng); own = np.arange(F * P)
    o = np.where(rng.random((N, 8, 1, S, P)) < 0.6, 256 * rng.integers(-1, 2, (N, 8, 1, S, P)), o)
    r[:, ::2] = rng.choice(np.array([-1024, -1, 0, 1, 1024]), (N, 4, 16, F, P))
    for i in range(16): m[:, 1::2, i] = i % 3
    far = np.array([0, F * P - 1, V, V + F * P - 1])
    for q in range(N):
        for g in range(8):
            k = (g + q) & 7
            if k == 0: a[q, g] = own
            if k == 1: a[q, g] = own ^ 1
            if k == 2: a[q, g] = (own + 1) % (F * P)
            if k == 3: a[q, g] = V + own
            if k == 4: a[q, g] = rng.choice(far, F * P)
            if k == 5: a[q, g, :P] = own[:P]
            if k == 6: a[q, g, :(F - 1) * P] = own[:(F - 1) * P]
            if k == 7:
                t = rng.integers(0, 5, F * P)
                a[q, g] = np.where(t == 0, own, np.where(t == 1, own ^ 1, np.where(t == 2, V + own, np.where(t == 3, rng.choice(far, F * P), a[q, g]))))
    x = int(rng.integers(0, N)); w = (x - 1) % N; mine = own.reshape(F, P)
    b = 2 * (rng.permutation(P) & 1) - 1; climb = rng.permutation(P) < P // 2
    odd = 2 * rng.permutation(P // 2)[:4] + 1; evn = 2 * rng.permutation(P // 2)[:8]; t = np.array([1, -1])
    d1, d2, low, mid, up, led = odd[:2], odd[2:], evn[:2], evn[2:4], evn[4:6], evn[6:]
    for z in (d1, d2, up, led): b[z] = t
    for z in (low, mid): b[z] = -t
    lead = np.where(climb & (np.arange(F)[:, None] > 0), -b, b); to = np.where(climb, np.arange(P), mine)
    for z in (low, mid, up): lead[:, z] = -t
    lead[:, led] = t
    to[:, up] = led; to[:, led] = mine[:, led]; to[:, mid] = d1
    to[:, low] = d2; to[0, low] = mid; to[F - 1, low] = mine[F - 1, low]
    for z in (d1, d2): to[:, z] = z; to[F - 1, z] = mine[F - 1, low]
    inner = (np.arange(F) > 0) & (np.arange(F) < F - 1)
    run = np.where(inner, -1020, 1024)[None, :, None] - 3 * (np.arange(16) & 1)[:, None, None]
    to = to.reshape(-1)
    for q in (x, w):
        r[q] = lead * (1024 - rng.integers(0, 4, r[q].shape)); o[q] = 256 * b; m[q] = 2
        r[q][..., d1] = t * run; r[q][..., d2] = t * (run - 1)
        a[q] = to if q == x else V + to
    return pack(r, o, v, m, a)
def setup_inputs_crowd(rng):
    r, o, v, m, a = parts(rng); two = rng.permutation(P)[:2]; x, y = int(two[0]), int(two[1])
    for q in range(N):
        for g in range(7):
            w = int(rng.integers(0, F * P)); one = int(rng.integers(0, F * P))
            if g == 6: w = F * P - 1
            if g in (0, 1, 6): a[q, g] = w
            if g == 2: a[q, g] = w; a[q, g, one] = V + one
            if g == 3: a[q, g] = V + w
            if g == 4: a[q, g] = V + w; a[q, g, one] = one
        a[q, 5] = np.where(rng.random(F * P) < 0.5, x, V + y); a[q, 5, x] = x
        r[q, 5, :, F - 1] = rng.integers(-50, 51, (16, P)); r[q, 5, :, 0, x] = 900; r[q, 5, :, 0, y] = 100
        if q % 2: r[q, 5, 3, 0, y] = 1020
    return pack(r, o, v, m, a)
def setup_inputs_ties(rng):
    r, o, v, m, a = parts(rng)
    b = (rng.integers(500, 1001, 16) * (2 * rng.integers(0, 2, 16) - 1))[None, None, :, None, None]
    k = rng.choice(np.array([0, 7, 8, 9, 10, 16]), (N, 8, 1, F, P)); place = np.argsort(np.argsort(rng.random(r.shape), axis=2), axis=2)
    dist = np.where(place < k, 4, 5 + rng.integers(0, 2, (N, 8, 1, F, P)))
    r = b + dist * (2 * rng.integers(0, 2, r.shape) - 1); r[:, :, :, F - 1] = b[:, :, :, 0]
    o = rng.integers(-1, 2, o.shape); m[:, :4] = 0
    a = rng.integers(0, 2, a.shape) * V + rng.integers(0, (F - 1) * P, a.shape)
    return pack(r, o, v, m, a)
def check_ranges(d):
    bad = []
    for k, lo, hi in (("r0", -1024, 1024), ("oc", -256, 256), ("mu", 0, 2), ("opp", 0, V + F * P - 1), ("stake", 0.25, 4)):
        w = np.asarray(d[k]).astype(np.float64)
        if not (np.min(w) >= lo and np.max(w) <= hi): bad.append("range of " + k)
        if k in ("oc", "mu") and np.any(w != np.floor(w)): bad.append("whole numbers of " + k)
    w = np.asarray(d["opp"]).astype(np.int64)
    if np.any((w >= F * P) & (w < V)): bad.append("opp names an empty slot")
    return bad
def both(R):
    w = R.reshape(N, 8, 16, V)
    return np.concatenate([w, np.roll(w, -1, axis=0)], axis=3)
def met(R, a):
    return np.take_along_axis(both(R), a[:, :, None, :], 3).reshape(N, 8, 16, -1, P)
def reference(r0, oc, stake, mu, opp):
    R = np.zeros((N, 8, 16, S, P), np.int64); R[:, :, :, :F] = r0.astype(np.int64).reshape(N, 8, 16, F, P)
    o = oc.astype(np.float64).reshape(N, 8, 16, S, P); v = stake.astype(np.float64).reshape(N, 8, 16, S, P)
    m = mu.astype(np.float64).reshape(N, 8, 16, 2 * (S - 1)); al, ga = m[..., :S - 1], m[..., S - 1:]
    L = np.zeros((N, 8, V), np.int64); L[:, :, :F * P] = np.stack([gentries(b) for b in opp])
    for rnd in range(RO):
        n = F + rnd
        a = L[:, :, :n * P].copy(); home = a < V
        c = np.where(home, np.take_along_axis(L, np.where(home, a, 0), 2), a)
        oneself = ((c < V) & ((c & (P - 1)) == np.tile(np.arange(P), n))).reshape(N, 8, n, P)
        me = R[:, :, :, n - 1].copy()
        dist = np.abs(met(R, c) - me[:, :, :, None, :])
        best = np.full((N, 8, 16, P), 2 ** 17, np.int64); pick = a[:, :, :P].copy(); c = c.reshape(N, 8, n, P)
        for k in range(n):
            nearer = np.add.reduce((dist[:, :, :, k] < best).astype(np.int64), axis=2)
            win = (nearer >= 9) & ~oneself[:, :, k]
            best = np.where(win[:, :, None, :], dist[:, :, :, k], best); pick = np.where(win, c[:, :, k], pick)
        L[:, :, n * P:(n + 1) * P] = np.where(pick >= V, V, 0) + (n - 1) * P + (pick & (P - 1))
        R[:, :, :, n] = (me + np.roll(me, -1, axis=1)) >> 1
        n = n + 1
        for sweep in range(SW):
            e = o[:, :, :, :n] - np.clip(R[:, :, :, :n] - met(R, L[:, :, :n * P]), -256, 256)
            d = e.copy()
            for s in range(1, n): d[:, :, :, s] += 0.5 * al[..., s - 1, None] * d[:, :, :, s - 1]
            x = np.floor(d)
            for s in range(n - 2, -1, -1): x[:, :, :, s] += 0.5 * ga[..., s, None] * x[:, :, :, s + 1]
            R[:, :, :, :n] += np.floor(0.0625 * x).astype(np.int64)
    z = (R - met(R, L)) * 2.0 ** -8
    y = np.add.reduce(v * (0.5 + 0.5 * np.tanh(0.5 * z)), axis=3)
    return {"y": y.reshape(N, 128, P).astype(np.float32), "yr": R.reshape(N, 128, V).astype(np.float32), "yo": np.stack([gtable(b) for b in L[:, :, F * P:]]).astype(np.float32)}

def check_inputs(d):
    bad = list(check_ranges(d))
    if not bad:
        for name, y in reference(**d).items():
            for q in range(N):
                v = np.abs(np.asarray(y[q], np.float64)); s = np.sqrt(np.mean(v * v))
                if v.max() > 11 * s or s < 2.0 ** 0: bad.append('%s of rank %d is uneven or too small' % (name, q))
    return bad

@@ -1,0 +1,580 @@
+import numpy as np
+from concourse.mybir import AluOpType, ActivationFunctionType
+
+P, S, F0, RO = 256, 8, 5, 3
+NC, CS = 4, 64
+CW = S * CS
+AW = NC * CW
+FAR = 2 * AW
+M = 12582912.0
+H16 = "float16"
+ROUTE = [[8, 8, 0, 0]] + [[8, 4, 0, 0] for _ in range(6)]
+DVE_FLOOR = (3,)
+ORDER1 = "G0 beats C0 step G1 cb C1 pk cn tn G2 cw C2 F0 G3 F1 C3 B0 F2 oi B1 U0 F3 B2 L3 U1 B3 U2 U3"
+ORDER2 = "G0 C0 G1 C1 F0 G2 C2 F1 B0 G3 C3 F2 B1 U0 F3 B2 L3 U1 B3 U2 U3"
+
+SCRATCH = {}
+for _i in range(7):
+    SCRATCH["W%d" % _i] = ("sbuf", [128, FAR + 8], "float32")
+for _i in range(8):
+    SCRATCH["ps%d" % _i] = ("psum", [128, 512], "float32")
+for _n in (6, 7, 8):
+    SCRATCH["ta%d" % _n] = ("sbuf", [128, CS * _n], "float32")
+    SCRATCH["tc%d" % _n] = ("sbuf", [128, CS * _n], "float32")
+    SCRATCH["tk%d" % _n] = ("sbuf", [128, CS * _n], "bfloat16")
+SCRATCH.update({
+    "r0s": ("sbuf", [128, 5, 256], "int32"), "ops": ("sbuf", [128, 80], "int32"), "ocs": ("sbuf", [128, 2048], "bfloat16"),
+    "sts": ("sbuf", [128, 8, 256], "bfloat16"), "mus": ("sbuf", [128, 16], "bfloat16"),
+    "lrep": ("sbuf", [128, 1288], "int32"), "lrep5": ("sbuf", [128, 264], "int32"),
+    "i16": ("sbuf", [128, 128], H16), "oa": ("sbuf", [128, 80], H16),
+    "colx": ("sbuf", [128, 144], "float32"), "rowi": ("sbuf", [128, 8], "int32"), "rowf": ("sbuf", [128, 8], "float32"),
+    "pt0": ("sbuf", [128, 80], "float32"), "ptab": ("sbuf", [128, 80], "float32"),
+    "ib": ("sbuf", [128, 128], "bfloat16"), "ih": ("sbuf", [128, 128], H16), "nh": ("sbuf", [128, 128], H16),
+    "i32": ("sbuf", [128, 128], "float32"), "sh": ("sbuf", [128, 128], "float32"), "sh1": ("sbuf", [128, 128], "float32"),
+    "sh2": ("sbuf", [128, 128], "float32"), "ez": ("sbuf", [128, 144], H16),
+    "muf": ("sbuf", [128, 32], "float32"), "one": ("sbuf", [128, 64], "float32"),
+    "xa": ("sbuf", [128, 96], "int32"), "xb": ("sbuf", [128, 96], "int32"), "xc": ("sbuf", [128, 96], "int32"),
+    "xd": ("sbuf", [128, 96], "float32"), "xe": ("sbuf", [128, 96], "float32"), "xf": ("sbuf", [128, 96], "float32"),
+    "xg": ("sbuf", [128, 96], "float32"), "xh": ("sbuf", [128, 96], "float32"), "xv": ("sbuf", [128, 96], "float32"),
+    "ya": ("sbuf", [128, 80], "int32"), "yb": ("sbuf", [128, 80], "int32"), "yc": ("sbuf", [128, 80], "float32"),
+    "yd": ("sbuf", [128, 80], "float32"), "ye": ("sbuf", [128, 80], "float32"), "yf": ("sbuf", [128, 5, 16], "float32"),
+    "hm": ("sbuf", [128, 80], "float32"), "ci": ("sbuf", [128, 96], "int32"),
+    "gl": ("sbuf", [128, 80], "uint16"), "lst": ("sbuf", [128, 128], "uint16"), "cl": ("sbuf", [128, 112], "uint16"),
+    "pk": ("sbuf", [128, 48], "uint16"), "oi": ("sbuf", [128, 48], "int32"), "yos": ("sbuf", [128, 48], "float32"),
+    "cb": ("sbuf", [128, 128], H16), "cn": ("sbuf", [128, 128], H16),
+    "bb": ("sbuf", [128, 8, 128], H16), "pp": ("sbuf", [128, 1024], H16), "pr": ("sbuf", [128, 256], H16),
+    "me": ("sbuf", [128, 256], "float32"), "mer": ("sbuf", [128, 256], "float32"), "rn": ("sbuf", [128, 256], "float32"),
+    "td": ("sbuf", [128, 1792], "float32"), "lt": ("sbuf", [128, 21 * 256], H16),
+    "tq": ("sbuf", [128, 2048], "bfloat16"), "cq": ("sbuf", [128, 2048], "bfloat16"),
+    "tn": ("sbuf", [128, 256], "bfloat16"), "cw": ("sbuf", [128, 256], "bfloat16"),
+    "d1": ("sbuf", [128, 2048], "float32"), "d2": ("sbuf", [128, 1024], "float32"), "d3": ("sbuf", [128, 2048], "float32"),
+    "rc": ("sbuf", [128, 2048], "float32"), "xs": ("sbuf", [128, 2048], "float32"), "yrs": ("sbuf", [128, 8, 256], "float32"), "ys": ("sbuf", [128, 256], "float32"),
+})
+SEMAPHORES = (["cv", "ca", "cp", "cg", "l_op", "l_r0", "l_mu", "l_lr", "l_oc", "l_st", "l_l5", "l_out", "sent"]
+              + ["arr%d" % i for i in range(7)] + ["hop%d_%d" % (i, c) for i in range(7) for c in range(NC)])
+
+
+def sent_slots(i):
+    return min(F0 + i // 2, S - 1)
+
+
+def ways(i, c):
+    n = sent_slots(i)
+    return min(ROUTE[i][c], n) * CS, n * CS
+
+
+def helper_of(src, dst, topo, T):
+    for h in topo.cores_of(src):
+        if h != src and topo.die(h) != topo.die(src) and T.rank_of(h) is None and topo.may_write(h, dst):
+            return h
+    return None
+
+
+def bits(mask):
+    return bin(mask).count("1")
+
+
+def helper_program(g, core, src, dst, T, topo):
+    rid, pid, _ = topo.addr(dst)
+    mask = topo.mask(core, dst)
+    hop = topo.mask(src, core) & ~topo.mask(src, dst)
+    total = 0
+    for i in range(7):
+        w = T["W%d" % i]
+        for c in range(NC):
+            n = ways(i, c)[0]
+            if n:
+                g.wait_ge(T.sem["hop%d_%d" % (i, c)], bits(hop))
+                g.remote_dma(w[:, AW + c * CW:AW + c * CW + n], w[:, c * CW:c * CW + n], T.sem["arr%d" % i], T.sem["sent"], pid, rid, mask)
+                total += bits(mask)
+    if total:
+        g.wait_ge(T.sem["sent"], total)
+
+
+def rank_program(g, core, T, topo):
+    cores = list(T.cores)
+    N = len(cores)
+    rank = T.rank_of(core)
+    if rank is None:
+        for r in range(N):
+            if helper_of(cores[r], cores[(r - 1) % N], topo, T) == core:
+                helper_program(g, core, cores[r], cores[(r - 1) % N], T, topo)
+        return
+    dst = cores[(rank - 1) % N]
+    src = cores[(rank + 1) % N]
+    helper = helper_of(core, dst, topo, T)
+    A = AluOpType
+    AF = ActivationFunctionType
+    Q = {"v": g.vector, "a": g.scalar, "p": g.tensor, "g": g, "s": g.sync}
+    count = {}
+    seen = {q: {} for q in Q}
+    writer, readers, bank = {}, {}, {}
+    toks = [None]
+
+    def width(name):
+        return int(np.prod(SCRATCH[name][1][1:]))
+
+    def V(name, a=0, b=None, step=1):
+        if b is None:
+            b = width(name)
+        if step > 0:
+            return (T[name][:, a:b:step] if step > 1 else T[name][:, a:b], name, np.arange(a, b, step))
+        return (T[name][:, b - 1:(a - 1 if a else None):-1], name, np.arange(a, b))
+
+    def V3(name, r0, r1, c0, c1):
+        w = SCRATCH[name][1][2]
+        cols = (np.arange(r0, r1)[:, None] * w + np.arange(c0, c1)[None, :]).ravel()
+        return (T[name][:, r0, c0:c1] if r1 == r0 + 1 else T[name][:, r0:r1, c0:c1], name, cols)
+
+    def IND(win, off):
+        return (win[0].indirect(off[0]), win[1], win[2], off)
+
+    def wait(q, tok):
+        if seen[q].get(tok[0], 0) < tok[1]:
+            Q[q].wait_ge(T.sem[tok[0]], int(tok[1]))
+            seen[q][tok[0]] = tok[1]
+
+    def order(q, sem, n, reads, writes):
+        need = {}
+
+        def add(t, same):
+            if t is not None and (same or t[2] != q):
+                need[t[0]] = max(need.get(t[0], 0), t[1])
+        tok = (sem, count.get(sem, 0) + n, q)
+        rd = []
+        for r in reads:
+            rd.append(r)
+            if len(r) == 4:
+                rd.append(r[3])
+        for v, is_w in [(r, False) for r in rd] + [(w, True) for w in writes]:
+            name, cols = v[1], v[2]
+            if name not in writer:
+                writer[name] = np.zeros(width(name), np.int64)
+                readers[name] = {}
+            for k in np.unique(writer[name][cols]):
+                add(toks[k], q in "va" or (q != "p" and not is_w))
+            if is_w:
+                for arr in readers[name].values():
+                    k = int(arr[cols].max())
+                    add(toks[k], q in "va")
+            if name[:2] == "ps":
+                for t in bank.get(name, {}).values():
+                    add(t, False)
+        for s_, c_ in need.items():
+            wait(q, (s_, c_))
+        toks.append(tok)
+        k = len(toks) - 1
+        for r in rd:
+            readers[r[1]].setdefault(sem, np.zeros(width(r[1]), np.int64))[r[2]] = k
+        for w in writes:
+            writer[w[1]][w[2]] = k
+        for v in rd + list(writes):
+            if v[1][:2] == "ps":
+                bank.setdefault(v[1], {})[q] = tok
+        return tok
+
+    def done(ins, sem, n):
+        ins.then_inc(T.sem[sem], n)
+        count[sem] = count.get(sem, 0) + n
+
+    def sc(x):
+        return x if isinstance(x, (int, float)) or x is None else x[0]
+
+    def aps(*xs):
+        return [x for x in xs if isinstance(x, tuple)]
+
+    def ts(out, in0, s1, op0, s2=None, op1=None):
+        order("v", "cv", 1, aps(in0, s1, s2), [out])
+        if op1 is None:
+            done(g.vector.tensor_scalar(out[0], in0[0], sc(s1), None, op0), "cv", 1)
+        else:
+            done(g.vector.tensor_scalar(out[0], in0[0], sc(s1), sc(s2), op0, op1), "cv", 1)
+
+    def tt(out, in0, in1, op):
+        order("v", "cv", 1, [in0, in1], [out])
+        done(g.vector.tensor_tensor(out[0], in0[0], in1[0], op), "cv", 1)
+
+    def cp(out, in_):
+        order("v", "cv", 1, [in_], [out])
+        done(g.vector.tensor_copy(out[0], in_[0]), "cv", 1)
+
+    def fill(out, x):
+        order("v", "cv", 1, [], [out])
+        done(g.vector.memset(out[0], x), "cv", 1)
+
+    def scan(out, d0, d1):
+        order("v", "cv", 1, [d0, d1], [out])
+        done(g.vector.tensor_tensor_scan(out[0], d0[0], d1[0], 0.0, A.mult, A.add), "cv", 1)
+
+    def act(out, in_, func=AF.Identity, bias=0.0, scale=1.0):
+        order("a", "ca", 1, aps(in_, bias, scale), [out])
+        done(g.scalar.activation(out[0], in_[0], func, bias=sc(bias), scale=sc(scale)), "ca", 1)
+
+    def mms(items):
+        for k, (out, lt_, rhs, st, sp) in enumerate(items):
+            order("p", "cp", 1, [lt_, rhs], [out])
+            ins = g.tensor.matmul(out[0], lt_[0], rhs[0], st, sp)
+            if k == len(items) - 1:
+                done(ins, "cp", 1)
+
+    def iota(out, pattern, mult):
+        order("g", "cg", 1, [], [out])
+        if SCRATCH[out[1]][2] == "int32":
+            done(g.iota(out[0], pattern, 0, mult), "cg", 1)
+        else:
+            done(g.iota(out[0], pattern, 0, mult, allow_small_or_imprecise_dtypes=True), "cg", 1)
+
+    def dmas(sem, items):
+        n = 16 * len(items)
+        for q, o, i_, rd, wr in items:
+            order(q, sem, n, rd, wr)
+        for q, o, i_, rd, wr in items:
+            done(Q[q].dma_start(o, i_), sem, 16)
+
+    def send(i, c):
+        nh, n = ways(i, c)
+        a = c * CW
+        order("g", "sent", 0, [V("W%d" % i, a, a + n)], [])
+        w = T["W%d" % i]
+        if nh:
+            rid, pid, _ = topo.addr(helper)
+            mask = topo.mask(core, helper) & ~topo.mask(core, dst)
+            g.remote_dma(w[:, a:a + nh], w[:, a:a + nh], T.sem["hop%d_%d" % (i, c)], T.sem["sent"], pid, rid, mask)
+            count["sent"] = count.get("sent", 0) + bits(mask)
+        if nh < n:
+            rid, pid, _ = topo.addr(dst)
+            mask = topo.mask(core, dst)
+            g.remote_dma(w[:, AW + a + nh:AW + a + n], w[:, a + nh:a + n], T.sem["arr%d" % i], T.sem["sent"], pid, rid, mask)
+            count["sent"] = count.get("sent", 0) + bits(mask)
+
+    def arrived(i):
+        hs = helper_of(src, core, topo, T)
+        total = 0
+        for c in range(NC):
+            nh, n = ways(i, c)
+            total += (bits(topo.mask(hs, core)) if nh else 0) + (bits(topo.mask(src, core)) if nh < n else 0)
+        wait("v", ("arr%d" % i, total))
+
+    def W(i, a, b):
+        return V("W%d" % i, a, b)
+
+    def win(i, far=False):
+        return V("W%d" % i, 0, FAR + 8 if far else FAR)
+
+    E, Y, D, CUR = ("ps0", "ps1"), ("ps2", "ps3"), ("ps4", "ps5", "ps6"), "ps7"
+
+    dmas("l_op", [("s", T.ops[:], T.opp[:], [], [V("ops")])])
+    dmas("l_r0", [("a", T.r0s[:], T.r0[:], [], [V3("r0s", 0, 5, 0, 256)])])
+    dmas("l_lr", [("s" if i % 2 == 0 else "a", T.lrep[i::16, 8:], T.opp[:], [], [V("lrep", 8)] if i == 0 else []) for i in range(16)])
+    dmas("l_mu", [("a", T.mus[:, 0:14], T.mu[:], [], [V("mus", 0, 14)])])
+    dmas("l_oc", [("s", T.ocs[:], T.oc[:], [], [V("ocs")])])
+
+    iota(V("rowi", 0, 1), [[0, 1]], 1)
+    iota(V("colx"), [[1, 144]], 0)
+    iota(V("pt0"), [[0, 5], [16, 16]], 0)
+    fill(V("lrep", 0, 8), 2048)
+    fill(V("lrep5", 0, 8), 2048)
+    fill(V("one"), 1.0)
+    fill(V("pp"), 1.0)
+    for i in (0, 2, 4):
+        fill(W(i, FAR, FAR + 8), M + 262144.0)
+    row = V("rowf", 0, 1)
+    col = V("colx", 0, 128)
+    ts(V("rowi", 1, 2), V("rowi", 0, 1), 112, A.bitwise_and)
+    ts(V("rowi", 2, 3), V("rowi", 0, 1), 15, A.bitwise_and)
+    cp(row, V("rowi", 0, 1))
+    ts(V("rowf", 1, 2), V("rowi", 1, 2), 15.0, A.add)
+    cp(V("rowf", 2, 3), V("rowi", 2, 3))
+    ts(V("sh1"), col, row, A.subtract)
+    ts(V("ez"), V("colx"), V("rowf", 1, 2), A.is_equal)
+    ts(V("i16"), col, row, A.is_equal, 16.0, A.mult)
+    ts(V("sh2"), V("sh1"), -16.0, A.is_equal, 0.5, A.mult)
+    ts(V("sh"), V("sh1"), 112.0, A.is_equal, 0.5, A.mult)
+    ts(V("i32"), V("sh1"), 0.0, A.is_equal, 0.5, A.mult)
+    tt(V("sh2"), V("sh2"), V("sh"), A.add)
+    ts(V("ptab"), V("pt0"), V("rowf", 2, 3), A.add)
+    tt(V("sh"), V("sh2"), V("i32"), A.add)
+
+    def more_constants():
+        ts(V("ib"), col, row, A.is_equal)
+        ts(V("ih"), col, row, A.is_equal)
+        ts(V("nh"), col, row, A.is_equal, -1.0, A.mult)
+
+    def EZ(i):
+        return V("ez", 15 - i, 143 - i)
+
+    def table_list(o, w, mult, const):
+        ts(V("ya", 0, w), o, 15, A.bitwise_and)
+        ts(V("yb", 0, w), o, 4, A.arith_shift_right, 127 if w == 80 else 15, A.bitwise_and)
+        ts(V("hm", 0, w), o, 2047.5, A.is_lt)
+        ts(V("yc", 0, w), V("ya", 0, w), float(mult), A.mult, float(const + 8), A.add)
+        ts(V("oa", 0, w), o, -2048.0, A.add, 0.0, A.max)
+        tt(V("yd", 0, w), V("yc", 0, w), V("yb", 0, w), A.add)
+        tt(V("ye", 0, w), V("yd", 0, w), V("hm", 0, w), A.mult)
+        cp(V("gl", 0, w), V("ye", 0, w))
+
+    def candidates(w, table, out, ps):
+        ts(V("lt", 0, 16 * w), IND(V(table), V("gl", 0, w)), -2048.0, A.add)
+        mms([(V(ps, 0, w), V("i16"), V("oa", 0, w), True, False)]
+            + [(V(ps, 0, w), EZ(i), V("lt", i, 16 * w, 16), False, i == 15) for i in range(16)])
+        yield
+        ts(out, V(ps, 0, w), 0.0625, A.mult, 2048.0, A.add)
+
+    def describe(w, lead, k0):
+        c = V("ci", 0, w)
+        nk = (w - lead) // 16
+        ts(V("xa", 0, w), c, 192, A.bitwise_and)
+        ts(V("xc", 0, w), c, 2303, A.bitwise_and)
+        ts(V("xd", 0, w), V("xa", 0, w), 7.0, A.mult, -float(FAR), A.add)
+        ts(V("xb", 0, w), c, 2, A.arith_shift_right, 448, A.bitwise_and)
+        tt(V("xe", 0, w), V("xc", 0, w), V("xd", 0, w), A.add)
+        tt(V("xv", lead, w), V("xc", lead, w), V("ptab", 0, w - lead), A.not_equal)
+        tt(V("xg", lead, w), V("xe", lead, w), V("xb", lead, w), A.add)
+        b0 = (k0 + 1) * 16 - lead
+        tt(V3("bb", k0, k0 + nk, 0, 16), V("xc", lead, w), V("ptab", 0, w - lead), A.is_equal)
+        tt(V("xh", lead, w), V("xg", lead, w), V("xv", lead, w), A.mult)
+        ts(V("cb", b0, b0 + w), V("xe", 0, w), FAR - 2048.0, A.add)
+        ts(V("cl", k0 * 16, (k0 + nk) * 16), V("xh", lead, w), float(FAR), A.add)
+        ts(V("cn", b0, b0 + w), V("xc", 0, w), -2048.0, A.add)
+
+    def tables(n):
+        one = V("one")
+        for s in range(n):
+            act(V("tk%d" % n, s, CS * n, n), one, scale=V("muf", 16 + s, 17 + s))
+        for s in range(n):
+            act(V("ta%d" % n, s, CS * n, n), one, scale=V("muf", s - 1, s) if s else 0.0)
+        for s in range(n):
+            act(V("tc%d" % n, s, CS * n, n), one, scale=V("muf", 7 + s, 8 + s) if s < n - 1 else 0.0)
+
+    def newest(i, f, c):
+        v = W(i, c * CW + (f - 1) * CS, c * CW + f * CS)
+        act(V("mer", c * CS, (c + 1) * CS), v, bias=-M)
+
+    def new_rating(i, f):
+        mms([(V(CUR, 256, 512), V("sh"), V("mer"), True, True)])
+        act(V("me"), V("mer"), bias=M)
+        yield
+        ts(V("rn"), V(CUR, 256, 512), -0.25, A.add, M, A.add)
+        for c in range(NC):
+            act(W(i, c * CW + f * CS, c * CW + (f + 1) * CS), V("rn", c * CS, (c + 1) * CS))
+
+    def own_copy(i, n):
+        for c in range(NC):
+            act(V("rc", c * CW, c * CW + n * CS), W(i, c * CW, c * CW + n * CS))
+
+    def preload(n, c):
+        e = E[c % 2]
+        mms([(V(e, 0, CS * n), V("ib"), V("tk%d" % n), True, False)]
+            + [(V(e, s, CS * n, n), V("ib"), V("ocs", s * P + c * CS, s * P + (c + 1) * CS), False, False) for s in range(n)])
+
+    o = V("ops")
+    table_list(o, 80, 80, 0)
+    for c in range(NC):
+        ts(W(0, c * CW, c * CW + F0 * CS), V3("r0s", 0, 5, c * CS, (c + 1) * CS), M, A.add)
+        send(0, c)
+        newest(0, F0, c)
+    rating = new_rating(0, F0)
+    next(rating)
+    gen = candidates(80, "lrep", V("ci", 16, 96), Y[0])
+    next(gen)
+    next(rating, None)
+    cp(V("ci", 0, 16), V("ops", 0, 16))
+    ts(V("muf", 0, 14), V("mus", 0, 14), 0.5, A.mult)
+    ts(V("muf", 17, 24), V("mus", 0, 7), 2.0, A.not_equal, -0.25, A.mult)
+    fill(V("muf", 16, 17), -0.25)
+    more_constants()
+    next(gen, None)
+    describe(96, 16, 0)
+    ts(V("xa", 0, 80), o, 192, A.bitwise_and)
+    ts(V("xc", 0, 80), o, 2303, A.bitwise_and)
+    ts(V("xd", 0, 80), V("xa", 0, 80), 7.0, A.mult)
+    ts(V("xb", 0, 80), o, 2, A.arith_shift_right, 448, A.bitwise_and)
+    tt(V("xe", 0, 80), V("xd", 0, 80), V("xc", 0, 80), A.add)
+    tt(V3("yf", 0, 5, 0, 16), V("xe", 0, 80), V("xb", 0, 80), A.add)
+    for c in range(NC):
+        cp(V("lst", c * 32, c * 32 + 20), V3("yf", 0, 5, 4 * c, 4 * c + 4))
+    tables(6)
+    own_copy(0, F0)
+    dmas("l_st", [("s", T.sts[:], T.stake[:], [V("lst", 0, 2)], [V3("sts", 0, 8, 0, 256)])])
+
+    def sweep_parts(i, n, ng):
+        def G(c):
+            tt(V("tq", c * CW, c * CW + ng * CS), IND(win(i), V("lst", c * 32, c * 32 + 4 * ng)), V("rc", c * CW, c * CW + ng * CS), A.subtract)
+
+        def C(c):
+            ts(V("cq", c * CW, c * CW + ng * CS), V("tq", c * CW, c * CW + ng * CS), 256.0, A.min, -256.0, A.max)
+
+        def PE(c):
+            mms([(V(E[c % 2], s, CS * n, n), V("ib"), V("cq", c * CW + s * CS, c * CW + (s + 1) * CS), False, s == n - 1) for s in range(ng)])
+
+        def PN(c):
+            mms([(V(E[c % 2], n - 1, CS * n, n), V("ib"), V("cw", c * CS, (c + 1) * CS), False, True)])
+
+        def Fw(c):
+            d1 = V("d1", c * CW, c * CW + n * CS)
+            scan(d1, V("ta%d" % n), V(E[c % 2], 0, n * CS))
+            if c + 2 < NC:
+                preload(n, c + 2)
+            if c not in DVE_FLOOR:
+                d2 = V("d2", (c % 2) * CW, (c % 2) * CW + n * CS)
+                act(d2, d1, bias=M)
+                act(V("d3", c * CW, c * CW + n * CS), d2, bias=-M)
+
+        def FL(c):
+            ts(V("d3", c * CW, c * CW + n * CS), V("d1", c * CW, c * CW + n * CS), M, A.add, -M, A.add)
+
+        def B(c):
+            scan(V("xs", c * CW, c * CW + n * CS, -1), V("tc%d" % n, 0, n * CS, -1), V("d3", c * CW, c * CW + n * CS, -1))
+            for s in range(n):
+                act(V(Y[c % 2], s * CS, (s + 1) * CS), V("xs", c * CW + s, c * CW + n * CS, n), bias=-(0.5 - 2.0 ** -12), scale=0.0625)
+
+        def U(c):
+            tt(W(i + 1, c * CW, c * CW + n * CS), W(i, c * CW, c * CW + n * CS), V(Y[c % 2], 0, n * CS), A.add)
+            send(i + 1, c)
+        did = set()
+
+        def run(text, extra):
+            for w in text.split():
+                if w in extra:
+                    extra[w]()
+                else:
+                    {"G": G, "C": C, "F": Fw, "L": FL, "B": B, "U": U}[w[0]](int(w[1]))
+                did.add(w)
+                for c in range(NC):
+                    free = c < 2 or "F%d" % (c - 2) in did
+                    if free and "C%d" % c in did and "P%d" % c not in did:
+                        PE(c)
+                        did.add("P%d" % c)
+                    if ng < n and "P%d" % c in did and "cw" in did and "N%d" % c not in did:
+                        PN(c)
+                        did.add("N%d" % c)
+        return run
+
+    for r in range(RO):
+        f = F0 + r
+        n = f + 1
+        i = 2 * r
+        run = sweep_parts(i, n, f)
+
+        def gather(k):
+            t = V("td", k * P, (k + 1) * P)
+            tt(t, IND(win(i, True), V("cl", k * 16, (k + 1) * 16)), V("me"), A.subtract)
+            if k < f - 1:
+                act(V(D[k // 2], (k % 2) * P, (k % 2 + 1) * P), t, AF.Abs)
+            if k > 0:
+                act(V("xs", k * P, (k + 1) * P), t, AF.Abs)
+
+        def compare(j, k):
+            off = P * (k * (k - 1) // 2 + j)
+            tt(V("lt", off, off + P), V("xs", k * P, (k + 1) * P), V(D[j // 2], (j % 2) * P, (j % 2 + 1) * P), A.is_lt)
+
+        def counts(k):
+            off = P * (k * (k - 1) // 2)
+            mms([(V(Y[k % 2], 0, 16 * k), EZ(x), V("lt", off + x, off + P * k, 16), x == 0, x == 15) for x in range(16)])
+
+        def beats(k):
+            ts(V3("bb", k, k + 1, 16, 16 * (k + 1)), V(Y[k % 2], 0, 16 * k), 8.5, A.is_lt)
+
+        def step(k):
+            w = 16 * (k + 1)
+            if k == 0:
+                cp(V("pp", 0, w), V3("bb", 0, 1, 0, w))
+            else:
+                tt(V("pp", k * 128, k * 128 + w), V(CUR, 0, w), V3("bb", k, k + 1, 0, w), A.mult)
+            mms([(V(CUR, 0, w + 16), V("ih"), V("pp", k * 128, k * 128 + w + 16), True, False)]
+                + [(V(CUR, w, w + 16), V("nh"), V("pp", k * 128 + 16 * j, k * 128 + 16 * j + 16), False, j == k) for j in range(k + 1)])
+
+        def choose(h, table):
+            w = 16 * (f + 1)
+            tt(V("pr", h * 128, h * 128 + w), V(CUR, 0, w), V(table, 0, w), A.mult)
+            mms([(V(D[h], 0, 16), V("ih"), V("pr", h * 128 + 16 * j, h * 128 + 16 * j + 16), j == 0, j == f) for j in range(f + 1)])
+
+        preload(n, 0)
+        preload(n, 1)
+        step(0)
+        arrived(i)
+        gather(0)
+        gather(1)
+        gather(2)
+        for k in range(1, f):
+            if k + 2 < f:
+                gather(k + 2)
+            for j in range(k):
+                compare(j, k)
+                if k >= 2 and j == k - 2:
+                    beats(k - 1)
+            if k >= 2:
+                step(k - 1)
+            counts(k)
+        pk = V("pk", 16 * r, 16 * r + 16)
+        oi = V("oi", 16 * r, 16 * r + 16)
+        run(ORDER1, {
+            "beats": lambda: beats(f - 1), "step": lambda: step(f - 1), "cb": lambda: choose(0, "cb"), "cn": lambda: choose(1, "cn"),
+            "pk": lambda: ts(pk, V(D[0], 0, 16), 2048.0 + (f - 1) * CS, A.add),
+            "tn": lambda: tt(V("tn"), IND(win(i), pk), V("rn"), A.subtract),
+            "cw": lambda: ts(V("cw"), V("tn"), 256.0, A.min, -256.0, A.max),
+            "oi": lambda: ts(oi, V(D[1], 0, 16), 2048.0 + (f - 1) * P, A.add)})
+        preload(n, 0)
+        preload(n, 1)
+        own_copy(i + 1, n)
+        for c in range(NC):
+            cp(V("lst", c * 32 + 4 * f, c * 32 + 4 * f + 4), V("pk", 16 * r + 4 * c, 16 * r + 4 * c + 4))
+        cp(V("yos", 16 * r, 16 * r + 16), oi)
+        if r == 0:
+            dmas("l_l5", [("s", T.lrep5[x::16, 8:], T.oi[:, 0:16], [oi], [V("lrep5", 8)] if x == 0 else []) for x in range(16)])
+        if r < RO - 1:
+            tables(n + 1)
+            table_list(oi, 16, 80 if r == 0 else 16, 64 if r == 0 else 0)
+            gen = candidates(16, "lrep" if r == 0 else "lrep5", V("ci", 0, 16), D[2])
+            next(gen)
+            next(gen, None)
+            describe(16, 0, f)
+        else:
+            ts(V("i32"), col, row, A.is_equal)
+            dmas("l_out", [("s", T.yo[:], T.yos[:], [V("yos")], [])])
+
+        arrived(i + 1)
+        sweep_parts(i + 1, n, n)(ORDER2, {})
+        if r < RO - 1:
+            for c in range(NC):
+                newest(i + 2, n, c)
+            for _ in new_rating(i + 2, n):
+                pass
+        own_copy(i + 2, n)
+    for c in range(NC):
+        act(V3("yrs", 0, 8, c * CS, (c + 1) * CS), W(6, c * CW, (c + 1) * CW), bias=-M)
+
+    dmas("l_out", [("s", T.yr[:], T.yrs[:], [V3("yrs", 0, 8, 0, 256)], [])])
+    arrived(6)
+
+    def GF(c):
+        t = V("d1", c * CW, (c + 1) * CW)
+        tt(t, IND(win(6), V("lst", c * 32, (c + 1) * 32)), V("rc", c * CW, (c + 1) * CW), A.subtract)
+        act(V("ps%d" % c), t, AF.Sigmoid, scale=-1.0 / 256)
+
+    def MF(c):
+        a = c * CW
+        if c < NC - 1:
+            tt(V("d3", a, a + CW), V("ps%d" % c), V3("sts", 0, 8, c * CS, (c + 1) * CS), A.mult)
+            mms([(V("ps%d" % (4 + c), 0, CS), V("i32"), V("d3", a + s * CS, a + (s + 1) * CS), s == 0, s == S - 1) for s in range(S)])
+        else:
+            tt(V("d3", a, a + 256), V("ps%d" % c, 0, 256), V3("sts", 0, 4, c * CS, (c + 1) * CS), A.mult)
+            tt(V(CUR, 0, 256), V("ps%d" % c, 256, 512), V3("sts", 4, 8, c * CS, (c + 1) * CS), A.mult)
+            tt(V("d3", a + 256, a + 384), V(CUR, 0, 128), V("d3", a, a + 128), A.add)
+            tt(V(CUR, 256, 384), V(CUR, 128, 256), V("d3", a + 128, a + 256), A.add)
+            tt(V("d3", a + 384, a + 448), V(CUR, 256, 320), V("d3", a + 256, a + 320), A.add)
+            tt(V(CUR, 384, 448), V(CUR, 320, 384), V("d3", a + 320, a + 384), A.add)
+            tt(V("ys", c * CS, (c + 1) * CS), V(CUR, 384, 448), V("d3", a + 384, a + 448), A.add)
+    GF(0)
+    GF(1)
+    GF(2)
+    MF(0)
+    MF(1)
+    GF(3)
+    MF(2)
+    for c in range(NC - 1):
+        act(V("ys", c * CS, (c + 1) * CS), V("ps%d" % (4 + c), 0, CS))
+    MF(3)
+    dmas("l_out", [("a", T.y[:], T.ys[:], [V("ys")], [])])
+    for s_, c_ in count.items():
+        wait("g", (s_, c_))

@@ -1,181 +1,252 @@
 import numpy as np
+from concourse.bass import DstId, RemoteDMATransfer
 from concourse.mybir import AluOpType, ActivationFunctionType
 
-P, S, F0, RO = 256, 8, 5, 3
+P, S, F0, RO, N = 256, 8, 5, 3, 4
 NC, CS = 4, 64
-CW = S * CS
-AW = NC * CW
-FAR = 2 * AW
+CW = CS * S
+FAR = 2 * P * S
 M = 12582912.0
-H16 = "float16"
-ROUTE = [[8, 8, 0, 0]] + [[8, 4, 0, 0] for _ in range(6)]
-DVE_FLOOR = (3,)
-ORDER1 = "G0 beats C0 step G1 cb C1 pk cn tn G2 cw C2 F0 G3 F1 C3 B0 F2 oi B1 U0 F3 B2 L3 U1 B3 U2 U3"
-ORDER2 = "G0 C0 G1 C1 F0 G2 C2 F1 B0 G3 C3 F2 B1 U0 F3 B2 L3 U1 B3 U2 U3"
+M16 = M / 16
+K0 = (-0.5 + 2.0 ** -8) / 16
+EPS = 2.0 ** -12
+H16, B16, F32 = "float16", "bfloat16", "float32"
+PLACE = [0, 2, 1, 3]
+FIRST = {5: 5, 6: 3, 7: 4}
+RELAYED = [(0, 0), (0, 1)]
+AWAY = "ddpc"
+CYCLE, GATHER, PE_CYCLE, HOP, DMA_START, WRITE_START = 0.83, 1.4, 0.42, 100, 1500, 1800
+BATCH = 5
+WIDE = (8,)
+SCAN = [(), (), (), (2,), (), (2,)]
 
 SCRATCH = {}
-for _i in range(7):
-    SCRATCH["W%d" % _i] = ("sbuf", [128, FAR + 8], "float32")
+for _i in range(2):
+    SCRATCH["W%d" % _i] = ("sbuf", [128, FAR + S], F32)
 for _i in range(8):
-    SCRATCH["ps%d" % _i] = ("psum", [128, 512], "float32")
-for _n in (6, 7, 8):
-    SCRATCH["ta%d" % _n] = ("sbuf", [128, CS * _n], "float32")
-    SCRATCH["tc%d" % _n] = ("sbuf", [128, CS * _n], "float32")
-    SCRATCH["tk%d" % _n] = ("sbuf", [128, CS * _n], "bfloat16")
+    SCRATCH["ps%d" % _i] = ("psum", [128, 512], F32)
 SCRATCH.update({
-    "r0s": ("sbuf", [128, 5, 256], "int32"), "ops": ("sbuf", [128, 80], "int32"), "ocs": ("sbuf", [128, 2048], "bfloat16"),
-    "sts": ("sbuf", [128, 8, 256], "bfloat16"), "mus": ("sbuf", [128, 16], "bfloat16"),
-    "lrep": ("sbuf", [128, 1288], "int32"), "lrep5": ("sbuf", [128, 264], "int32"),
-    "i16": ("sbuf", [128, 128], H16), "oa": ("sbuf", [128, 80], H16),
-    "colx": ("sbuf", [128, 144], "float32"), "rowi": ("sbuf", [128, 8], "int32"), "rowf": ("sbuf", [128, 8], "float32"),
-    "pt0": ("sbuf", [128, 80], "float32"), "ptab": ("sbuf", [128, 80], "float32"),
-    "ib": ("sbuf", [128, 128], "bfloat16"), "ih": ("sbuf", [128, 128], H16), "nh": ("sbuf", [128, 128], H16),
-    "i32": ("sbuf", [128, 128], "float32"), "sh": ("sbuf", [128, 128], "float32"), "sh1": ("sbuf", [128, 128], "float32"),
-    "sh2": ("sbuf", [128, 128], "float32"), "ez": ("sbuf", [128, 144], H16),
-    "muf": ("sbuf", [128, 32], "float32"), "one": ("sbuf", [128, 64], "float32"),
-    "xa": ("sbuf", [128, 96], "int32"), "xb": ("sbuf", [128, 96], "int32"), "xc": ("sbuf", [128, 96], "int32"),
-    "xd": ("sbuf", [128, 96], "float32"), "xe": ("sbuf", [128, 96], "float32"), "xf": ("sbuf", [128, 96], "float32"),
-    "xg": ("sbuf", [128, 96], "float32"), "xh": ("sbuf", [128, 96], "float32"), "xv": ("sbuf", [128, 96], "float32"),
-    "ya": ("sbuf", [128, 80], "int32"), "yb": ("sbuf", [128, 80], "int32"), "yc": ("sbuf", [128, 80], "float32"),
-    "yd": ("sbuf", [128, 80], "float32"), "ye": ("sbuf", [128, 80], "float32"), "yf": ("sbuf", [128, 5, 16], "float32"),
-    "hm": ("sbuf", [128, 80], "float32"), "ci": ("sbuf", [128, 96], "int32"),
-    "gl": ("sbuf", [128, 80], "uint16"), "lst": ("sbuf", [128, 128], "uint16"), "cl": ("sbuf", [128, 112], "uint16"),
-    "pk": ("sbuf", [128, 48], "uint16"), "oi": ("sbuf", [128, 48], "int32"), "yos": ("sbuf", [128, 48], "float32"),
-    "cb": ("sbuf", [128, 128], H16), "cn": ("sbuf", [128, 128], H16),
-    "bb": ("sbuf", [128, 8, 128], H16), "pp": ("sbuf", [128, 1024], H16), "pr": ("sbuf", [128, 256], H16),
-    "me": ("sbuf", [128, 256], "float32"), "mer": ("sbuf", [128, 256], "float32"), "rn": ("sbuf", [128, 256], "float32"),
-    "td": ("sbuf", [128, 1792], "float32"), "lt": ("sbuf", [128, 21 * 256], H16),
-    "tq": ("sbuf", [128, 2048], "bfloat16"), "cq": ("sbuf", [128, 2048], "bfloat16"),
-    "tn": ("sbuf", [128, 256], "bfloat16"), "cw": ("sbuf", [128, 256], "bfloat16"),
-    "d1": ("sbuf", [128, 2048], "float32"), "d2": ("sbuf", [128, 1024], "float32"), "d3": ("sbuf", [128, 2048], "float32"),
-    "rc": ("sbuf", [128, 2048], "float32"), "xs": ("sbuf", [128, 2048], "float32"), "yrs": ("sbuf", [128, 8, 256], "float32"), "ys": ("sbuf", [128, 256], "float32"),
+    "ops": ("sbuf", [128, 80], "int32"), "mus": ("sbuf", [128, 16], B16), "lp": ("sbuf", [128, N, 96], H16),
+    "s32": ("sbuf", [128, N, 320], "int32"), "s16": ("sbuf", [128, N, 320], H16),
+    "so": ("sbuf", [128, N, 512], B16), "ss": ("sbuf", [128, N, 512], B16),
+    "dr": ("dram", [N, 128, 320], H16), "dc": ("dram", [N, 128, 512], B16), "ds": ("dram", [N, 128, 512], B16),
+    "r16": ("sbuf", [128, 1280], H16), "ocs": ("sbuf", [128, 2048], B16), "sts": ("sbuf", [128, 2048], B16),
+    "dyr": ("dram", [4 * N, 128, 128], F32), "lyr": ("sbuf", [128, 2 * N, 256], F32),
+    "sy": ("sbuf", [128, N, 64], F32), "ly": ("sbuf", [128, N, 64], F32), "zq": ("sbuf", [128, 516], F32),
+    "dyo": ("dram", [N, 128, 12], F32), "lyo": ("sbuf", [128, N, 12], F32),
+    "yos": ("sbuf", [128, 48], F32), "yo1": ("sbuf", [128, 48], F32), "yo2": ("sbuf", [128, 48], F32), "ys": ("sbuf", [128, 256], F32),
+    "colx": ("sbuf", [128, 224], F32), "colg": ("sbuf", [128, 128], F32), "rowi": ("sbuf", [128, 8], "int32"),
+    "rowf": ("sbuf", [128, 8], F32), "rowg": ("sbuf", [128, 8], F32), "ones": ("sbuf", [128, 516], B16),
+    "pt0": ("sbuf", [128, 80], F32), "ptab": ("sbuf", [128, 80], F32), "mk": ("sbuf", [128, 16], F32),
+    "ib": ("sbuf", [128, 128], B16), "nb": ("sbuf", [128, 128], B16), "i32": ("sbuf", [128, 128], F32),
+    "rot": ("sbuf", [128, 128], F32), "rot16": ("sbuf", [128, 128], B16), "sh": ("sbuf", [128, 128], F32), "sh2": ("sbuf", [128, 128], F32),
+    "t0": ("sbuf", [128, 128], F32), "t1": ("sbuf", [128, 128], F32), "t2": ("sbuf", [128, 128], F32),
+    "ez": ("sbuf", [128, 144], B16), "sel": ("sbuf", [128, 224], B16), "bo": ("sbuf", [128, 128], B16), "bi": ("sbuf", [128, 16, 128], B16),
+    "am": ("sbuf", [128, 29, 128], B16), "big": ("sbuf", [128, CW], B16), "qrt": ("sbuf", [128, P], B16),
+    "epw": ("sbuf", [128, CW], B16), "tc": ("sbuf", [128, CW], F32),
+    "ta": ("sbuf", [128, CW], F32), "og": ("sbuf", [128, CW], F32),
+    "l4": ("sbuf", [128, 64, 16], B16), "hz": ("sbuf", [128, 3, 64], F32), "hw": ("sbuf", [128, 8, 16], F32),
+    "muf": ("sbuf", [128, 64], F32), "ix": ("sbuf", [128, 96], H16), "ix0": ("sbuf", [128, 80], F32),
+    "xa": ("sbuf", [128, 80], "int32"), "xb": ("sbuf", [128, 80], "int32"), "xc": ("sbuf", [128, 80], "int32"), "xo": ("sbuf", [128, 80], "int32"),
+    "xd": ("sbuf", [128, 80], F32), "xe": ("sbuf", [128, 80], F32), "xf": ("sbuf", [128, 80], F32), "xg": ("sbuf", [128, 80], F32),
+    "xh": ("sbuf", [128, 80], F32), "hm": ("sbuf", [128, 80], F32), "co": ("sbuf", [128, 80], "int32"), "a8": ("sbuf", [128, 80], "int32"),
+    "a0": ("sbuf", [128, 16], "int32"),
+    "lh": ("sbuf", [128, 128], H16), "oa": ("sbuf", [128, 80], H16), "lrep": ("sbuf", [128, 1288], F32), "tb": ("sbuf", [128, 264], F32),
+    "gl": ("sbuf", [128, 80], "uint16"), "ln": ("sbuf", [128, 128], "uint16"), "cl": ("sbuf", [128, 112], "uint16"), "gi": ("sbuf", [128, 16], "uint16"),
+    "cb": ("sbuf", [128, 128], H16), "bb": ("sbuf", [128, 8, 128], H16), "pp": ("sbuf", [128, 7 * 128], H16), "pr": ("sbuf", [128, 3, 128], H16),
+    "mer": ("sbuf", [128, RO, P], F32), "mn": ("sbuf", [128, RO, P], F32), "rn": ("sbuf", [128, P], F32), "da": ("sbuf", [128, P], F32),
+    "td": ("sbuf", [128, 1792], F32), "xs": ("sbuf", [128, 1800], F32), "lt": ("sbuf", [128, 21 * 256], H16), "lc": ("sbuf", [128, 1280], H16),
+    "tq": ("sbuf", [128, 2048], B16), "cq": ("sbuf", [128, 2048], B16),
+    "do": ("sbuf", [128, P * S], F32), "rc": ("sbuf", [128, S, P], F32), "ow": ("sbuf", [128, 2048], F32),
+    "d1": ("sbuf", [128, 2048], F32), "d3": ("sbuf", [128, 2048], F32),
 })
-SEMAPHORES = (["cv", "ca", "cp", "cg", "l_op", "l_r0", "l_mu", "l_lr", "l_oc", "l_st", "l_l5", "l_out", "sent"]
-              + ["arr%d" % i for i in range(7)] + ["hop%d_%d" % (i, c) for i in range(7) for c in range(NC)])
-
-
-def sent_slots(i):
-    return min(F0 + i // 2, S - 1)
-
-
-def ways(i, c):
-    n = sent_slots(i)
-    return min(ROUTE[i][c], n) * CS, n * CS
-
-
-def helper_of(src, dst, topo, T):
-    for h in topo.cores_of(src):
-        if h != src and topo.die(h) != topo.die(src) and T.rank_of(h) is None and topo.may_write(h, dst):
-            return h
-    return None
+SEMAPHORES = (["cv", "ca", "cp", "cg", "sent", "l_op", "l_mu", "l_ss", "l_dr", "l_dc", "l_ds", "l_r", "l_oc", "l_st",
+               "a_lp", "a_r", "a_c", "a_s", "a_yo", "d_yo", "out"]
+              + ["h_c%d" % j for j in range(N)] + ["h_s%d" % j for j in range(N)] + ["h_y%d" % j for j in range(4 * N)]
+              + ["l_s%d" % j for j in range(N)] + ["l_o%d" % j for j in range(N)] + ["a_mn%d" % r for r in range(RO)]
+              + ["a_y%d" % j for j in range(N)] + ["d_yr%d" % k for k in range(4)] + ["a_yr%d" % k for k in range(4 * N)]
+              + ["w%d_%d" % (i, c) for i in range(6) for c in range(NC)])
 
 
 def bits(mask):
     return bin(mask).count("1")
 
 
-def helper_program(g, core, src, dst, T, topo):
-    rid, pid, _ = topo.addr(dst)
-    mask = topo.mask(core, dst)
-    hop = topo.mask(src, core) & ~topo.mask(src, dst)
+def helpers_of(src, topo, T):
+    return [h for h in topo.cores_of(src)
+            if topo.die(h) != topo.die(src) and T.rank_of(h) is None and all(topo.may_write(h, c) for c in T.cores)]
+
+
+def relayed(T, rank, topo):
+    others = [(rank + k) % N for k in range(1, N)]
+    hs = helpers_of(T.cores[rank], topo, T)
+    jobs = ([(T.so[:, q], "h_c%d" % q, q, T.dc[PLACE[rank]], "a_c") for q in others[1:]]
+            + [(T.ss[:, q], "h_s%d" % q, q, T.ds[PLACE[rank]], "a_s") for q in others]
+            + [(T.lyr[:, 2 * q + k, 128 * h:128 * h + 128], "h_y%d" % (4 * q + 2 * k + h), q,
+                T.lyr[:, 2 * rank + k, 128 * h:128 * h + 128], "a_yr%d" % (4 * rank + 2 * k + h)) for k, h in RELAYED for q in others])
+    return [(hs[k % len(hs)],) + job for k, job in enumerate(jobs)]
+
+
+def hop_mask(src, topo, T):
+    return topo.mask(src, helpers_of(src, topo, T)[0]) & ~topo.mask(src, [c for c in T.cores if c != src][0])
+
+
+def helper_program(g, core, rank, T, topo):
     total = 0
-    for i in range(7):
-        w = T["W%d" % i]
-        for c in range(NC):
-            n = ways(i, c)[0]
-            if n:
-                g.wait_ge(T.sem["hop%d_%d" % (i, c)], bits(hop))
-                g.remote_dma(w[:, AW + c * CW:AW + c * CW + n], w[:, c * CW:c * CW + n], T.sem["arr%d" % i], T.sem["sent"], pid, rid, mask)
-                total += bits(mask)
-    if total:
-        g.wait_ge(T.sem["sent"], total)
+    for h, here, sem, q, there, sem_there in relayed(T, rank, topo):
+        if h != core:
+            continue
+        rid, pid, _ = topo.addr(T.cores[q])
+        mask = topo.mask(core, T.cores[q])
+        g.wait_ge(T.sem[sem], bits(hop_mask(T.cores[rank], topo, T)))
+        g.remote_dma(there, here, T.sem[sem_there], T.sem["sent"], pid, rid, mask)
+        total += bits(mask)
+    g.wait_ge(T.sem["sent"], total)
+
+
+def issue(calls, Q, T):
+    for k, c in enumerate(calls):
+        c["next"] = []
+        for j in c["after"]:
+            calls[j]["next"].append(k)
+    todo = list(range(len(calls)))
+    while todo:
+        c = calls[todo[-1]]
+        open_ = [k for k in c["next"] + c["then"] if "way" not in calls[k]]
+        if open_:
+            todo += open_
+            continue
+        c["way"] = max([c["lat"] + calls[k]["way"] + HOP for k in c["next"]] + [c["busy"] + calls[k]["way"] for k in c["then"]], default=c["lat"])
+        c["left"], c["from"] = len(c["after"]), 0.0
+        todo.pop()
+    free = {q: 0.0 for q in list(Q) + ["x"]}
+    bank = {}
+    ready = [k for k, c in enumerate(calls) if not c["left"]]
+    line = []
+
+    def start(k, q):
+        c = calls[k]
+        t = max(free[q], c["from"])
+        for b in c["banks"]:
+            for x, j in bank.get(b, {}).items():
+                if x != q:
+                    t = max(t, calls[j]["end"] + HOP)
+        return t
+    while ready:
+        when = {(k, q): start(k, q) for k in ready for q in calls[k]["q"]}
+        k, q = min(when, key=lambda x: (when[x], x[1]))
+        k = max((j for j, x in when if x == q and when[j, q] <= when[k, q] + HOP / 2), key=lambda j: (calls[j].get("first", -99), calls[j]["way"], -j))
+        c = calls[k]
+        if len(c["q"]) > 1:
+            c["emit"], c["q"] = c["emit"][q], q
+        ready.remove(k)
+        for b in c["banks"]:
+            c["waits"] |= set(j for x, j in bank.setdefault(b, {}).items() if x != q)
+            bank[b][q] = k
+        c["end"] = when[k, q] + c["lat"]
+        if q != "x":
+            free[q] = when[k, q] + c["busy"]
+        line.append(k)
+        for j in c["next"]:
+            d = calls[j]
+            d["from"] = max(d["from"], c["end"] + (0 if q == d["q"] == "p" else HOP))
+            d["left"] -= 1
+            if not d["left"]:
+                ready.append(j)
+    needed = set(j for c in calls for j in c["waits"])
+    count, seen = {}, {q: {} for q in Q}
+
+    def wait(q, sem, n):
+        if seen[q].get(sem, 0) < n:
+            Q[q].wait_ge(T.sem[sem], int(n))
+            seen[q][sem] = n
+    for k in line:
+        c = calls[k]
+        if c["q"] != "x":
+            need = {}
+            for j in c["waits"]:
+                sem, n = calls[j]["token"]
+                need[sem] = max(need.get(sem, 0), n)
+            for sem, n in need.items():
+                wait(c["q"], sem, n)
+            ins = c["emit"]()
+            if "token" not in c:
+                sem = "c" + c["q"]
+                if k in needed:
+                    ins.then_inc(T.sem[sem], 1)
+                    count[sem] = count.get(sem, 0) + 1
+                c["token"] = (sem, count.get(sem, 0))
+        count[c["token"][0]] = max(count.get(c["token"][0], 0), c["token"][1])
+    for sem, n in count.items():
+        wait("g", sem, n)
 
 
 def rank_program(g, core, T, topo):
     cores = list(T.cores)
-    N = len(cores)
     rank = T.rank_of(core)
     if rank is None:
         for r in range(N):
-            if helper_of(cores[r], cores[(r - 1) % N], topo, T) == core:
-                helper_program(g, core, cores[r], cores[(r - 1) % N], T, topo)
+            if core in helpers_of(cores[r], topo, T):
+                helper_program(g, core, r, T, topo)
         return
-    dst = cores[(rank - 1) % N]
-    src = cores[(rank + 1) % N]
-    helper = helper_of(core, dst, topo, T)
+    others = [(rank + k) % N for k in range(1, N)]
     A = AluOpType
     AF = ActivationFunctionType
-    Q = {"v": g.vector, "a": g.scalar, "p": g.tensor, "g": g, "s": g.sync}
-    count = {}
-    seen = {q: {} for q in Q}
-    writer, readers, bank = {}, {}, {}
-    toks = [None]
+    calls, total = [], {}
+    writer, readers, grid = {}, {}, {}
+    sl = slice
 
-    def width(name):
-        return int(np.prod(SCRATCH[name][1][1:]))
+    def cells(name):
+        if name not in grid:
+            where, shape, _ = SCRATCH[name]
+            grid[name] = np.arange(shape[0]) if where == "dram" else np.arange(int(np.prod(shape[1:]))).reshape(shape[1:])
+            writer[name] = np.full((4, grid[name].size), -1)
+            readers[name] = []
+        return grid[name]
+
+    def X(name, *ix, parts=sl(0, 128)):
+        return (T[name][(parts,) + ix], name, np.ravel(cells(name)[ix]), sl(parts.start // 32, parts.stop // 32))
 
     def V(name, a=0, b=None, step=1):
         if b is None:
-            b = width(name)
+            b = cells(name).size
         if step > 0:
-            return (T[name][:, a:b:step] if step > 1 else T[name][:, a:b], name, np.arange(a, b, step))
-        return (T[name][:, b - 1:(a - 1 if a else None):-1], name, np.arange(a, b))
+            return X(name, sl(a, b, step) if step > 1 else sl(a, b))
+        return (T[name][:, b - 1:(a - 1 if a else None):-1], name, cells(name)[a:b], sl(0, 4))
 
-    def V3(name, r0, r1, c0, c1):
-        w = SCRATCH[name][1][2]
-        cols = (np.arange(r0, r1)[:, None] * w + np.arange(c0, c1)[None, :]).ravel()
-        return (T[name][:, r0, c0:c1] if r1 == r0 + 1 else T[name][:, r0:r1, c0:c1], name, cols)
+    def D(name, ix):
+        return (T[name][ix], name, np.ravel(cells(name)[ix]), sl(0, 4))
 
     def IND(win, off):
-        return (win[0].indirect(off[0]), win[1], win[2], off)
+        return (win[0].indirect(off[0]),) + win[1:] + (off,)
 
-    def wait(q, tok):
-        if seen[q].get(tok[0], 0) < tok[1]:
-            Q[q].wait_ge(T.sem[tok[0]], int(tok[1]))
-            seen[q][tok[0]] = tok[1]
-
-    def order(q, sem, n, reads, writes):
-        need = {}
-
-        def add(t, same):
-            if t is not None and (same or t[2] != q):
-                need[t[0]] = max(need.get(t[0], 0), t[1])
-        tok = (sem, count.get(sem, 0) + n, q)
-        rd = []
-        for r in reads:
-            rd.append(r)
-            if len(r) == 4:
-                rd.append(r[3])
-        for v, is_w in [(r, False) for r in rd] + [(w, True) for w in writes]:
-            name, cols = v[1], v[2]
-            if name not in writer:
-                writer[name] = np.zeros(width(name), np.int64)
-                readers[name] = {}
-            for k in np.unique(writer[name][cols]):
-                add(toks[k], q in "va" or (q != "p" and not is_w))
+    def note(q, emit, busy, reads, writes, lat=None, token=None, after=()):
+        k = len(calls)
+        deps, waits = set(after), set()
+        reads = [x for r in reads for x in ([r] if len(r) == 4 else [r[:4], r[4]])]
+        for v, is_w in [(r, False) for r in reads] + [(w, True) for w in writes]:
+            _, name, cols, parts = v
+            found = [int(j) for j in np.unique(writer[name][parts, cols]) if j >= 0]
             if is_w:
-                for arr in readers[name].values():
-                    k = int(arr[cols].max())
-                    add(toks[k], q in "va")
-            if name[:2] == "ps":
-                for t in bank.get(name, {}).values():
-                    add(t, False)
-        for s_, c_ in need.items():
-            wait(q, (s_, c_))
-        toks.append(tok)
-        k = len(toks) - 1
-        for r in rd:
-            readers[r[1]].setdefault(sem, np.zeros(width(r[1]), np.int64))[r[2]] = k
-        for w in writes:
-            writer[w[1]][w[2]] = k
-        for v in rd + list(writes):
-            if v[1][:2] == "ps":
-                bank.setdefault(v[1], {})[q] = tok
-        return tok
-
-    def done(ins, sem, n):
-        ins.then_inc(T.sem[sem], n)
-        count[sem] = count.get(sem, 0) + n
+                mark = np.zeros(writer[name].shape, bool)
+                mark[parts, cols] = True
+                found += [j for j, p_, c_ in readers[name] if mark[p_, c_].any()]
+                readers[name] = [x for x in readers[name] if not mark[x[1], x[2]].all()]
+            for j in found:
+                for x in calls[j]["mates"]:
+                    deps.add(x)
+                    if calls[x]["q"] != q or q in "ava" or (q != "p" and not is_w):
+                        waits.add(x)
+        for _, name, cols, parts in reads:
+            readers[name].append((k, parts, cols))
+        for _, name, cols, parts in writes:
+            writer[name][parts, cols] = k
+        c = {"q": q, "emit": emit, "busy": busy, "lat": busy if lat is None else lat, "after": deps - {k}, "waits": waits - {k}, "mates": [k], "then": [],
+             "banks": set(v[1] for v in reads + list(writes) if v[1][:2] == "ps")}
+        if token:
+            c["token"] = token
+        calls.append(c)
+        return k
 
     def sc(x):
         return x if isinstance(x, (int, float)) or x is None else x[0]
@@ -183,398 +254,533 @@ def rank_program(g, core, T, topo):
     def aps(*xs):
         return [x for x in xs if isinstance(x, tuple)]
 
+    def kind(v):
+        return SCRATCH[v[1]][2]
+
+    def cost(fixed, out, ins, two=False):
+        n = len(out[2])
+        if any(len(x) == 5 for x in ins):
+            return 50 + fixed + n * GATHER * CYCLE
+        k = 2 if two and all(x[1][:2] != "ps" for x in ins) else 1
+        if all(kind(x) in (H16, B16, "uint16") for x in [out] + ins):
+            k /= 2
+        return fixed + max(64, n * k) * CYCLE
+
     def ts(out, in0, s1, op0, s2=None, op1=None):
-        order("v", "cv", 1, aps(in0, s1, s2), [out])
-        if op1 is None:
-            done(g.vector.tensor_scalar(out[0], in0[0], sc(s1), None, op0), "cv", 1)
-        else:
-            done(g.vector.tensor_scalar(out[0], in0[0], sc(s1), sc(s2), op0, op1), "cv", 1)
+        args = (out[0], in0[0], sc(s1), sc(s2), op0) + (() if op1 is None else (op1,))
+        note("v", lambda: g.vector.tensor_scalar(*args), cost(15, out, [in0]), aps(in0, s1, s2), [out])
 
     def tt(out, in0, in1, op):
-        order("v", "cv", 1, [in0, in1], [out])
-        done(g.vector.tensor_tensor(out[0], in0[0], in1[0], op), "cv", 1)
+        note("v", lambda: g.vector.tensor_tensor(out[0], in0[0], in1[0], op), cost(15, out, [in0, in1], True), [in0, in1], [out])
 
     def cp(out, in_):
-        order("v", "cv", 1, [in_], [out])
-        done(g.vector.tensor_copy(out[0], in_[0]), "cv", 1)
+        note("v", lambda: g.vector.tensor_copy(out[0], in_[0]), cost(15, out, [in_]), [in_], [out])
 
     def fill(out, x):
-        order("v", "cv", 1, [], [out])
-        done(g.vector.memset(out[0], x), "cv", 1)
+        note("v", lambda: g.vector.memset(out[0], x), cost(15, out, []), [], [out])
 
     def scan(out, d0, d1):
-        order("v", "cv", 1, [d0, d1], [out])
-        done(g.vector.tensor_tensor_scan(out[0], d0[0], d1[0], 0.0, A.mult, A.add), "cv", 1)
+        note("v", lambda: g.vector.tensor_tensor_scan(out[0], d0[0], d1[0], 0.0, A.mult, A.add), cost(15, out, [d1]), [d0, d1], [out])
 
-    def act(out, in_, func=AF.Identity, bias=0.0, scale=1.0):
-        order("a", "ca", 1, aps(in_, bias, scale), [out])
-        done(g.scalar.activation(out[0], in_[0], func, bias=sc(bias), scale=sc(scale)), "ca", 1)
+    def act(out, in_, func=AF.Identity, bias=0.0, scale=1.0, more=0):
+        note("a", lambda: g.scalar.activation(out[0], in_[0], func, bias=sc(bias), scale=sc(scale)),
+             30 + more + max(64, len(out[2])) * CYCLE, aps(in_, bias, scale), [out])
+
+    def move(out, in_, bias=0.0):
+        note("av", {"a": lambda: g.scalar.activation(out[0], in_[0], AF.Identity, bias=bias, scale=1.0),
+                    "v": lambda: g.vector.tensor_scalar(out[0], in_[0], bias, None, A.add)}, 25 + max(64, len(out[2])) * CYCLE, [in_], [out])
+
+    def in_turn(ks):
+        for j, k in zip(ks, ks[1:]):
+            calls[j]["then"].append(k)
 
     def mms(items):
-        for k, (out, lt_, rhs, st, sp) in enumerate(items):
-            order("p", "cp", 1, [lt_, rhs], [out])
-            ins = g.tensor.matmul(out[0], lt_[0], rhs[0], st, sp)
-            if k == len(items) - 1:
-                done(ins, "cp", 1)
+        def emit():
+            for out, lt_, rhs, st, sp in items:
+                ins = g.tensor.matmul(out[0], lt_[0], rhs[0], st, sp)
+            return ins
+        note("p", emit, sum(8 + max(64, len(x[2][2])) * PE_CYCLE * (4 if kind(x[1]) == F32 else 1) for x in items),
+             [v for x in items for v in x[1:3]], [x[0] for x in items])
 
     def iota(out, pattern, mult):
-        order("g", "cg", 1, [], [out])
-        if SCRATCH[out[1]][2] == "int32":
-            done(g.iota(out[0], pattern, 0, mult), "cg", 1)
+        more = {} if kind(out) == "int32" else {"allow_small_or_imprecise_dtypes": True}
+        note("g", lambda: g.iota(out[0], pattern, 0, mult, **more), 130 + 2 * len(out[2]) * CYCLE, [], [out])
+
+    def dmas(sem, items, kib, after=()):
+        total[sem] = total.get(sem, 0) + 16 * len(items)
+        first = len(calls)
+        for q, o, i_ in items:
+            def emit(q=q, o=o, i_=i_):
+                Q[q].dma_start(o[0] if isinstance(o, tuple) else o, i_[0] if isinstance(i_, tuple) else i_).then_inc(T.sem[sem], 16)
+            note(q, emit, 60, aps(i_), aps(o), DMA_START + 3 * kib, (sem, total[sem]), after)
+        for k in range(first, len(calls)):
+            calls[k]["mates"] = list(range(first, len(calls)))
+        return len(calls) - 1
+
+    def remote(to, out, in_, sem, mask):
+        rid, pid, _ = topo.addr(to)
+        total["sent"] = total.get("sent", 0) + bits(mask)
+        return note("g", lambda: g.remote_dma(out, in_[0], T.sem[sem], T.sem["sent"], pid, rid, mask), 250, [in_], [], token=("sent", total["sent"]))
+
+    def send(q, out, in_, sem):
+        return remote(cores[q], out[0], in_, sem, topo.mask(core, cores[q]))
+
+    def hop(sem, in_):
+        h, there = [x[:2] for x in relayed(T, rank, topo) if x[2] == sem][0]
+        return remote(h, there, in_, sem, hop_mask(core, topo, T))
+
+    def lands(sem, places, after, kib, hops=1):
+        n = sum(bits(topo.mask(cores[q], core)) for _, q in places)
+        note("x", None, 0, [], [v for v, _ in places], hops * WRITE_START + 10 * kib, (sem, n), after)
+
+    Q = {"v": g.vector, "a": g.scalar, "p": g.tensor, "g": g, "s": g.sync}
+
+    def rows(j, k=1):
+        return sl(32 * j, 32 * (j + k))
+
+    def W(i, ix, parts=sl(0, 128)):
+        return X("W%d" % (i % 2), ix, parts=parts)
+
+    def win(i):
+        return V("W%d" % (i % 2))
+
+    def chunk(c, away=0):
+        return sl(away * P * S + c * CW, away * P * S + (c + 1) * CW)
+
+    def along(s, a=0, b=P):
+        return sl(a * S + s, b * S, S)
+
+    def slot(name, a, b=None):
+        return V(name, a * P, (a + 1 if b is None else b) * P)
+
+    def own(i, s):
+        return X("rc", s) if i == 0 else X("ow", along(s))
+
+    def mu(k):
+        return V("muf", k, k + 1)
+
+    moves = []
+    for x in range(N):
+        y = PLACE[(PLACE.index(x) + 1) % N]
+        if moves and moves[-1][0] % 2 == moves[-1][1] % 2 == 0 and moves[-1][2] == 1 and y == moves[-1][1] + 1:
+            moves[-1][2] = 2
         else:
-            done(g.iota(out[0], pattern, 0, mult, allow_small_or_imprecise_dtypes=True), "cg", 1)
+            moves.append([x, y, 1])
+    DB, XB, DIST, CUR, TURN = ("ps0", "ps1", "ps2", "ps3"), ("ps4", "ps5"), ("ps4", "ps5", "ps6"), "ps7", ("ps6", "ps7")
 
-    def dmas(sem, items):
-        n = 16 * len(items)
-        for q, o, i_, rd, wr in items:
-            order(q, sem, n, rd, wr)
-        for q, o, i_, rd, wr in items:
-            done(Q[q].dma_start(o, i_), sem, 16)
-
-    def send(i, c):
-        nh, n = ways(i, c)
-        a = c * CW
-        order("g", "sent", 0, [V("W%d" % i, a, a + n)], [])
-        w = T["W%d" % i]
-        if nh:
-            rid, pid, _ = topo.addr(helper)
-            mask = topo.mask(core, helper) & ~topo.mask(core, dst)
-            g.remote_dma(w[:, a:a + nh], w[:, a:a + nh], T.sem["hop%d_%d" % (i, c)], T.sem["sent"], pid, rid, mask)
-            count["sent"] = count.get("sent", 0) + bits(mask)
-        if nh < n:
-            rid, pid, _ = topo.addr(dst)
-            mask = topo.mask(core, dst)
-            g.remote_dma(w[:, AW + a + nh:AW + a + n], w[:, a + nh:a + n], T.sem["arr%d" % i], T.sem["sent"], pid, rid, mask)
-            count["sent"] = count.get("sent", 0) + bits(mask)
-
-    def arrived(i):
-        hs = helper_of(src, core, topo, T)
-        total = 0
-        for c in range(NC):
-            nh, n = ways(i, c)
-            total += (bits(topo.mask(hs, core)) if nh else 0) + (bits(topo.mask(src, core)) if nh < n else 0)
-        wait("v", ("arr%d" % i, total))
-
-    def W(i, a, b):
-        return V("W%d" % i, a, b)
-
-    def win(i, far=False):
-        return V("W%d" % i, 0, FAR + 8 if far else FAR)
-
-    E, Y, D, CUR = ("ps0", "ps1"), ("ps2", "ps3"), ("ps4", "ps5", "ps6"), "ps7"
-
-    dmas("l_op", [("s", T.ops[:], T.opp[:], [], [V("ops")])])
-    dmas("l_r0", [("a", T.r0s[:], T.r0[:], [], [V3("r0s", 0, 5, 0, 256)])])
-    dmas("l_lr", [("s" if i % 2 == 0 else "a", T.lrep[i::16, 8:], T.opp[:], [], [V("lrep", 8)] if i == 0 else []) for i in range(16)])
-    dmas("l_mu", [("a", T.mus[:, 0:14], T.mu[:], [], [V("mus", 0, 14)])])
-    dmas("l_oc", [("s", T.ocs[:], T.oc[:], [], [V("ocs")])])
+    dmas("l_op", [("s", V("ops"), T.opp[:])], 40)
+    dmas("l_mu", [("a", V("mus", 0, 14), T.mu[:])], 40)
+    for k, j in enumerate(others + [rank]):
+        dmas("l_s%d" % j, [("sa"[k % 2], X("s32", j), T.r0[rows(j), :])], 200 * (k + 2))
+    for k, j in enumerate(others[1:] + others[:1]):
+        dmas("l_o%d" % j, [("sa"[k % 2], X("so", j), T.oc[rows(j), :])], 1000 + 128 * (k + 1))
+    dmas("l_dc", [("a", D("dc", PLACE[rank]), T.oc[rows(rank), :])], 128)
+    for k, c in enumerate(calls):
+        c["first"] = -k
 
     iota(V("rowi", 0, 1), [[0, 1]], 1)
-    iota(V("colx"), [[1, 144]], 0)
-    iota(V("pt0"), [[0, 5], [16, 16]], 0)
-    fill(V("lrep", 0, 8), 2048)
-    fill(V("lrep5", 0, 8), 2048)
-    fill(V("one"), 1.0)
+    iota(V("colx"), [[1, 224]], 0)
+    iota(V("colg"), [[16, 8], [0, 16]], 0)
+    iota(V("pt0"), [[0, 5], [128, 16]], 0)
+    iota(V("ix0"), [[256, 5], [16, 16]], 0)
+    row, col, one = V("rowf", 0, 1), V("colx", 0, 128), V("ones", 0, CS)
+    fill(X("lp", rank, sl(88, 96)), 0.0)
     fill(V("pp"), 1.0)
-    for i in (0, 2, 4):
-        fill(W(i, FAR, FAR + 8), M + 262144.0)
-    row = V("rowf", 0, 1)
-    col = V("colx", 0, 128)
-    ts(V("rowi", 1, 2), V("rowi", 0, 1), 112, A.bitwise_and)
-    ts(V("rowi", 2, 3), V("rowi", 0, 1), 15, A.bitwise_and)
-    cp(row, V("rowi", 0, 1))
-    ts(V("rowf", 1, 2), V("rowi", 1, 2), 15.0, A.add)
-    cp(V("rowf", 2, 3), V("rowi", 2, 3))
-    ts(V("sh1"), col, row, A.subtract)
-    ts(V("ez"), V("colx"), V("rowf", 1, 2), A.is_equal)
-    ts(V("i16"), col, row, A.is_equal, 16.0, A.mult)
-    ts(V("sh2"), V("sh1"), -16.0, A.is_equal, 0.5, A.mult)
-    ts(V("sh"), V("sh1"), 112.0, A.is_equal, 0.5, A.mult)
-    ts(V("i32"), V("sh1"), 0.0, A.is_equal, 0.5, A.mult)
-    tt(V("sh2"), V("sh2"), V("sh"), A.add)
-    ts(V("ptab"), V("pt0"), V("rowf", 2, 3), A.add)
-    tt(V("sh"), V("sh2"), V("i32"), A.add)
+    fill(V("ones"), 1.0)
+    for k, x in enumerate((112, 15, 16, 96)):
+        ts(V("rowi", k + 1, k + 2), V("rowi", 0, 1), x, A.bitwise_and)
+    cp(V("rowf", 0, 5), V("rowi", 0, 5))
+    ts(V("rowf", 5, 6), V("rowf", 4, 5), 32.0 * rank, A.not_equal, 1000.0, A.mult)
+    ts(V("rowf", 6, 7), V("rowf", 5, 6), row, A.add, 96.0 - 32 * rank, A.add)
+    ts(V("sel"), V("colx"), V("rowf", 6, 7), A.is_equal)
+    ts(V("ib"), col, row, A.is_equal)
+    ts(V("bo"), V("colg"), V("rowf", 1, 2), A.is_equal)
+    ts(V("mk"), V("colx", 0, 16), V("rowf", 2, 3), A.is_equal)
+    for i in range(16):
+        act(X("bi", i), V("bo"), scale=V("mk", i, i + 1))
+    act(V("nb"), V("ib"), scale=-1.0)
+    act(X("am", 0), V("ib"), scale=0.0625)
+    act(V("i32"), V("ib"))
+    for s in range(F0 + 1, S):
+        act(W(0, along(s)), V("ones", 0, P), scale=M)
+    for s in range(F0, S):
+        act(V("tc", s, CW, S), one, scale=0.0)
+    ts(V("rowg", 0, 1), V("rowf", 1, 2), 15.0, A.add)
+    ts(V("rowg", 1, 2), V("rowf", 2, 3), 8.0, A.mult)
+    ts(V("rowg", 2, 3), V("rowf", 3, 4), 1.0 / 32, A.mult)
+    ts(V("rowg", 3, 4), V("rowf", 3, 4), -1.0 / 32, A.mult, 0.5, A.add)
+    for x, y, k in moves:
+        ts(X("rowg", sl(4, 5), parts=rows(y, k)), X("rowf", sl(0, 1), parts=rows(y, k)), 32.0 * (x - y), A.add)
+    ts(V("t0"), col, row, A.subtract)
+    ts(V("ez"), V("colx", 0, 144), V("rowg", 0, 1), A.is_equal, 0.0625, A.mult)
+    ts(V("ptab"), V("pt0"), V("rowg", 1, 2), A.add)
+    ts(V("ix", 16, 96), V("ix0"), V("rowf", 2, 3), A.add)
+    fill(V("ix", 0, 16), 1792.0)
+    fill(V("xs", 1792, 1800), 131072.0)
+    act(X("l4", sl(0, 64, 4)), V("ones", 0, P))
+    fill(V("lrep", 0, 8), 0.0)
+    fill(V("tb", P, P + 8), 0.0)
+    act(V("big"), V("ones", 0, CW), scale=M16)
+    act(V("qrt"), V("ones", 0, P), scale=-0.25)
+    act(V("epw"), V("ones", 0, CW), scale=EPS)
+    for i in range(2):
+        fill(W(i, sl(FAR, FAR + S)), M + 262144.0)
+    ts(V("t1"), V("t0"), -16.0, A.is_equal, V("rowg", 2, 3), A.mult)
+    ts(V("t2"), V("t0"), 0.0, A.is_equal, 0.5, A.mult)
+    tt(V("sh"), V("t1"), V("t2"), A.add)
+    ts(V("sh2"), V("t0"), 16.0, A.is_equal, V("rowg", 3, 4), A.mult)
+    ts(V("rot"), col, V("rowg", 4, 5), A.is_equal)
+    act(V("rot16"), V("rot"))
 
-    def more_constants():
-        ts(V("ib"), col, row, A.is_equal)
-        ts(V("ih"), col, row, A.is_equal)
-        ts(V("nh"), col, row, A.is_equal, -1.0, A.mult)
+    o = V("ops")
+    ts(V("xa"), o, 255, A.bitwise_and)
+    ts(V("xc"), o, 2303, A.bitwise_and)
+    ts(V("xb"), o, 8, A.arith_shift_right, 7, A.bitwise_and)
+    ts(V("xd"), V("xa"), 7.0, A.mult, -2048.0, A.add)
+    tt(V("xe"), V("xc"), V("xb"), A.add)
+    cp(X("lp", rank, sl(80, 94)), V("mus", 0, 14))
+    tt(X("lp", rank, sl(0, 80)), V("xd"), V("xe"), A.add)
+    mask = topo.mask(core, cores[others[0]])
+    total["sent"] = bits(mask)
+    spread = RemoteDMATransfer(dst_ids=[DstId(rid=a[0], pnc=a[1]) for a in (topo.addr(cores[q]) for q in others)], dma_engine_mask=mask,
+                               remote_sem=T.sem["a_lp"], srcs=[X("lp", rank)[0]], dsts=[X("lp", rank)[0] for _ in others])
+    k0 = note("g", lambda: g.remote_dma_fused([spread], local_sem=T.sem["sent"]), 1500, [X("lp", rank)], [], token=("sent", total["sent"]))
+    lands("a_lp", [(X("lp", q), q) for q in others], [k0], 100)
+    for j in others + [rank]:
+        cp(X("s16", j), X("s32", j))
+    ks = [send(j, D("dr", PLACE[rank]), X("s16", j), "a_r") for j in others]
+    for k in ks:
+        calls[k]["after"].add(k0)
+    lands("a_r", [(D("dr", PLACE[q]), q) for q in others], ks, 240)
+    dmas("l_dr", [("s", D("dr", PLACE[rank]), X("s16", rank))], 80)
+    dmas("l_r", [("s", V("r16"), D("dr", sl(None)))], 320)
+    ko = [hop("h_c%d" % j, X("so", j)) for j in others[1:]] + [send(others[0], D("dc", PLACE[rank]), X("so", others[0]), "a_c")]
+    for k in ko:
+        calls[k]["after"].update(ks)
+    lands("a_c", [(D("dc", PLACE[q]), q) for q in others], ko, 256, 2)
+    k1 = dmas("l_oc", [("s", V("ocs"), D("dc", sl(None)))], 512)
+    note("g", lambda: g.affine_select(V("zq")[0], V("ones")[0], [[1, 516]], A.is_equal, 0.0, -4, -4), 1000, [V("ones")], [V("zq")], after=ko)
+    dmas("l_ss", [("s", X("ss", j), T.stake[rows(j), :]) for j in others], 384, [k1])
+    dmas("l_ds", [("s", D("ds", PLACE[rank]), T.stake[rows(rank), :])], 128, [k1])
 
     def EZ(i):
         return V("ez", 15 - i, 143 - i)
 
-    def table_list(o, w, mult, const):
-        ts(V("ya", 0, w), o, 15, A.bitwise_and)
-        ts(V("yb", 0, w), o, 4, A.arith_shift_right, 127 if w == 80 else 15, A.bitwise_and)
-        ts(V("hm", 0, w), o, 2047.5, A.is_lt)
-        ts(V("yc", 0, w), V("ya", 0, w), float(mult), A.mult, float(const + 8), A.add)
-        ts(V("oa", 0, w), o, -2048.0, A.add, 0.0, A.max)
-        tt(V("yd", 0, w), V("yc", 0, w), V("yb", 0, w), A.add)
-        tt(V("ye", 0, w), V("yd", 0, w), V("hm", 0, w), A.mult)
-        cp(V("gl", 0, w), V("ye", 0, w))
+    def AM(s, t):
+        return X("am", 0 if s == t else 1 + s * (s - 1) // 2 + t)
 
-    def candidates(w, table, out, ps):
-        ts(V("lt", 0, 16 * w), IND(V(table), V("gl", 0, w)), -2048.0, A.add)
-        mms([(V(ps, 0, w), V("i16"), V("oa", 0, w), True, False)]
-            + [(V(ps, 0, w), EZ(i), V("lt", i, 16 * w, 16), False, i == 15) for i in range(16)])
-        yield
-        ts(out, V(ps, 0, w), 0.0625, A.mult, 2048.0, A.add)
+    def factors(s, on):
+        for t in range(s - 1, -1, -1):
+            if on == "v":
+                ts(AM(s, t), AM(s, t + 1), mu(t), A.mult)
+            else:
+                act(AM(s, t), AM(s, t + 1), scale=mu(t))
 
-    def describe(w, lead, k0):
-        c = V("ci", 0, w)
-        nk = (w - lead) // 16
-        ts(V("xa", 0, w), c, 192, A.bitwise_and)
-        ts(V("xc", 0, w), c, 2303, A.bitwise_and)
-        ts(V("xd", 0, w), V("xa", 0, w), 7.0, A.mult, -float(FAR), A.add)
-        ts(V("xb", 0, w), c, 2, A.arith_shift_right, 448, A.bitwise_and)
-        tt(V("xe", 0, w), V("xc", 0, w), V("xd", 0, w), A.add)
-        tt(V("xv", lead, w), V("xc", lead, w), V("ptab", 0, w - lead), A.not_equal)
-        tt(V("xg", lead, w), V("xe", lead, w), V("xb", lead, w), A.add)
-        b0 = (k0 + 1) * 16 - lead
-        tt(V3("bb", k0, k0 + nk, 0, 16), V("xc", lead, w), V("ptab", 0, w - lead), A.is_equal)
-        tt(V("xh", lead, w), V("xg", lead, w), V("xv", lead, w), A.mult)
-        ts(V("cb", b0, b0 + w), V("xe", 0, w), FAR - 2048.0, A.add)
-        ts(V("cl", k0 * 16, (k0 + nk) * 16), V("xh", lead, w), float(FAR), A.add)
-        ts(V("cn", b0, b0 + w), V("xc", 0, w), -2048.0, A.add)
+    def candidates(w, k0, table, ps):
+        cp(V("lc", 0, 16 * w), IND(V(table), V("gl", 0, w)))
+        mms([(V(ps, 0, w), V("ib"), V("oa", 0, w), True, False)]
+            + [(V(ps, 0, w), EZ(i), V("lc", i, 16 * w, 16), False, i == 15) for i in range(16)])
+        nk = w // 16
+        own_ = X("bb", sl(k0, k0 + nk) if nk > 1 else k0, sl(0, 16))
+        ts(V("co", 0, w), V(ps, 0, w), 2048.0, A.add)
+        ts(V("a8", 0, w), V("co", 0, w), 4088, A.bitwise_and)
+        tt(own_, V("a8", 0, w), V("ptab", 0, w), A.is_equal)
+        ts(V("xf", 0, w), own_, float(FAR), A.mult)
+        tt(V("xg", 0, w), V("xf", 0, w), V("co", 0, w), A.max)
+        cp(V("cl", k0 * 16, k0 * 16 + w), V("xg", 0, w))
+        cp(V("cb", (k0 + 1) * 16, (k0 + 1) * 16 + w), V("a8", 0, w))
 
-    def tables(n):
-        one = V("one")
-        for s in range(n):
-            act(V("tk%d" % n, s, CS * n, n), one, scale=V("muf", 16 + s, 17 + s))
-        for s in range(n):
-            act(V("ta%d" % n, s, CS * n, n), one, scale=V("muf", s - 1, s) if s else 0.0)
-        for s in range(n):
-            act(V("tc%d" % n, s, CS * n, n), one, scale=V("muf", 7 + s, 8 + s) if s < n - 1 else 0.0)
+    def tables(s):
+        act(V("tc", s, CW, S), one, scale=mu(7 + s))
+        act(V("epw", s, CW, S), one, scale=mu(16 + s), bias=EPS)
 
-    def newest(i, f, c):
-        v = W(i, c * CW + (f - 1) * CS, c * CW + f * CS)
-        act(V("mer", c * CS, (c + 1) * CS), v, bias=-M)
+    def preload(i, c):
+        mms([(V(DB[c]), V("ib"), V("ones", 0, CW), True, False)])
+        act(V(DB[c]), V("og") if c in SCAN[i] else X("do", chunk(c)))
 
-    def new_rating(i, f):
-        mms([(V(CUR, 256, 512), V("sh"), V("mer"), True, True)])
-        act(V("me"), V("mer"), bias=M)
-        yield
-        ts(V("rn"), V(CUR, 256, 512), -0.25, A.add, M, A.add)
-        for c in range(NC):
-            act(W(i, c * CW + f * CS, c * CW + (f + 1) * CS), V("rn", c * CS, (c + 1) * CS))
+    mms([(V(CUR, 0, 96), V("sel", 96 - 32 * PLACE[q], 224 - 32 * PLACE[q]), X("lp", q), k == 0, k == N - 1) for k, q in enumerate([rank] + others)])
+    cp(V("lh", 0, 80), V(CUR, 0, 80))
+    ts(V("xo"), V(CUR, 0, 80), 2048.0, A.add)
+    ts(V("muf", 0, 14), V(CUR, 80, 94), 0.5, A.mult)
+    ts(V("muf", 16, 23), V(CUR, 87, 94), -EPS / 2, A.mult)
+    ts(V("muf", 24, 31), V(CUR, 87, 94), 0.25, A.mult)
+    for b in range(3):
+        blocks = range(6 * b, min(6 * b + 6, 16))
+        mms([(V(DIST[b], 80 * (i - 6 * b), 80 * (i - 6 * b + 1)), X("bi", i), V("lh", 0, 80), True, True) for i in blocks])
+        (cp if b == 1 else act)(V("lrep", 8 + 480 * b, 8 + 480 * b + 80 * len(blocks)), V(DIST[b], 0, 80 * len(blocks)))
+    ts(V("xa"), V("xo"), 3, A.arith_shift_right, 15, A.bitwise_and)
+    ts(V("xb"), V("xo"), 7, A.arith_shift_right, 15, A.bitwise_and)
+    ts(V("xc"), V("xo"), 7, A.bitwise_and)
+    ts(V("hm"), V("lh", 0, 80), 0.0, A.is_lt)
+    ts(V("xd"), V("xa"), 80.0, A.mult, 8.0, A.add)
+    ts(V("xe"), V("xc"), 16.0, A.mult)
+    tt(V("xf"), V("xd"), V("xb"), A.add)
+    tt(V("xg"), V("xf"), V("xe"), A.add)
+    tt(V("xh"), V("xg"), V("hm"), A.mult)
+    cp(V("gl"), V("xh"))
+    ts(V("oa"), V("lh", 0, 80), 0.0, A.max)
+    ts(V("a0"), V("xo", 0, 16), 4088, A.bitwise_and)
+    cp(V("cb", 0, 16), V("a0"))
+    cp(V("ln", 0, 80), V("xo"))
+    candidates(80, 0, "lrep", DIST[2])
+    for s in range(F0 + 1):
+        factors(s, "a")
+    for s in range(F0):
+        tables(s)
 
-    def own_copy(i, n):
-        for c in range(NC):
-            act(V("rc", c * CW, c * CW + n * CS), W(i, c * CW, c * CW + n * CS))
-
-    def preload(n, c):
-        e = E[c % 2]
-        mms([(V(e, 0, CS * n), V("ib"), V("tk%d" % n), True, False)]
-            + [(V(e, s, CS * n, n), V("ib"), V("ocs", s * P + c * CS, s * P + (c + 1) * CS), False, False) for s in range(n)])
-
-    o = V("ops")
-    table_list(o, 80, 80, 0)
+    for b in range(3):
+        mms([(V(DB[b], 0, min(512, 1280 - 512 * b)), V("rot16"), V("r16", 512 * b, min(512 * b + 512, 1280)), True, True)])
+    act(X("rc", F0 - 1), slot("r16", F0 - 1), bias=M)
+    act(X("rc", sl(0, 2)), slot("r16", 0, 2), bias=M)
+    act(X("rc", sl(2, 4)), slot("r16", 2, 4), bias=M)
+    for s in range(F0):
+        ts(W(0, along(s)), slot("r16", s), M, A.add)
+        away = W(0, along(s, P, 2 * P)), V(DB[s // 2], (s % 2) * P, (s % 2 + 1) * P)
+        if s < F0 - 1:
+            act(away[0], away[1], bias=M)
+        else:
+            ts(away[0], away[1], M, A.add)
+    ts(V("muf", 32, 32 + F0), V("muf", 24, 24 + F0), K0 - 0.5, A.add)
+    fill(V("muf", 32 + F0, 40), K0 - 0.5)
+    tt(V("muf", 41, 48), V("muf", 0, 7), V("muf", 32, 39), A.mult)
+    tt(V("muf", 49, 56), V("muf", 33, 40), V("muf", 41, 48), A.subtract)
+    for s in range(S):
+        act(V("ta", s, CW, S), one, scale=mu(s - 1) if s else 0.0)
+        act(X("d3", along(s)), slot("ocs", s), scale=0.0625, bias=mu(48 + s if s else 32))
     for c in range(NC):
-        ts(W(0, c * CW, c * CW + F0 * CS), V3("r0s", 0, 5, c * CS, (c + 1) * CS), M, A.add)
-        send(0, c)
-        newest(0, F0, c)
-    rating = new_rating(0, F0)
-    next(rating)
-    gen = candidates(80, "lrep", V("ci", 16, 96), Y[0])
-    next(gen)
-    next(rating, None)
-    cp(V("ci", 0, 16), V("ops", 0, 16))
-    ts(V("muf", 0, 14), V("mus", 0, 14), 0.5, A.mult)
-    ts(V("muf", 17, 24), V("mus", 0, 7), 2.0, A.not_equal, -0.25, A.mult)
-    fill(V("muf", 16, 17), -0.25)
-    more_constants()
-    next(gen, None)
-    describe(96, 16, 0)
-    ts(V("xa", 0, 80), o, 192, A.bitwise_and)
-    ts(V("xc", 0, 80), o, 2303, A.bitwise_and)
-    ts(V("xd", 0, 80), V("xa", 0, 80), 7.0, A.mult)
-    ts(V("xb", 0, 80), o, 2, A.arith_shift_right, 448, A.bitwise_and)
-    tt(V("xe", 0, 80), V("xd", 0, 80), V("xc", 0, 80), A.add)
-    tt(V3("yf", 0, 5, 0, 16), V("xe", 0, 80), V("xb", 0, 80), A.add)
-    for c in range(NC):
-        cp(V("lst", c * 32, c * 32 + 20), V3("yf", 0, 5, 4 * c, 4 * c + 4))
-    tables(6)
-    own_copy(0, F0)
-    dmas("l_st", [("s", T.sts[:], T.stake[:], [V("lst", 0, 2)], [V3("sts", 0, 8, 0, 256)])])
+        scan(X("do", chunk(c)), V("ta"), X("d3", chunk(c)))
 
-    def sweep_parts(i, n, ng):
-        def G(c):
-            tt(V("tq", c * CW, c * CW + ng * CS), IND(win(i), V("lst", c * 32, c * 32 + 4 * ng)), V("rc", c * CW, c * CW + ng * CS), A.subtract)
+    def newest(r, view, bias):
+        act(X("mer", r), view, bias=bias)
+        k = send(others[-1], X("mn", r), X("mer", r), "a_mn%d" % r)
+        lands("a_mn%d" % r, [(X("mn", r), others[0])], [k], 128)
+        return k
+    k0 = newest(0, slot("r16", F0 - 1), 0.0)
+    ks = [hop("h_s%d" % j, X("ss", j)) for j in others]
+    for k in ks:
+        calls[k]["after"].add(k0)
+    lands("a_s", [(D("ds", PLACE[q]), q) for q in others], ks, 3000, 2)
+    dmas("l_st", [("s", V("sts"), D("ds", sl(None)))], 512)
 
-        def C(c):
-            ts(V("cq", c * CW, c * CW + ng * CS), V("tq", c * CW, c * CW + ng * CS), 256.0, A.min, -256.0, A.max)
-
-        def PE(c):
-            mms([(V(E[c % 2], s, CS * n, n), V("ib"), V("cq", c * CW + s * CS, c * CW + (s + 1) * CS), False, s == n - 1) for s in range(ng)])
-
-        def PN(c):
-            mms([(V(E[c % 2], n - 1, CS * n, n), V("ib"), V("cw", c * CS, (c + 1) * CS), False, True)])
-
-        def Fw(c):
-            d1 = V("d1", c * CW, c * CW + n * CS)
-            scan(d1, V("ta%d" % n), V(E[c % 2], 0, n * CS))
-            if c + 2 < NC:
-                preload(n, c + 2)
-            if c not in DVE_FLOOR:
-                d2 = V("d2", (c % 2) * CW, (c % 2) * CW + n * CS)
-                act(d2, d1, bias=M)
-                act(V("d3", c * CW, c * CW + n * CS), d2, bias=-M)
-
-        def FL(c):
-            ts(V("d3", c * CW, c * CW + n * CS), V("d1", c * CW, c * CW + n * CS), M, A.add, -M, A.add)
-
-        def B(c):
-            scan(V("xs", c * CW, c * CW + n * CS, -1), V("tc%d" % n, 0, n * CS, -1), V("d3", c * CW, c * CW + n * CS, -1))
-            for s in range(n):
-                act(V(Y[c % 2], s * CS, (s + 1) * CS), V("xs", c * CW + s, c * CW + n * CS, n), bias=-(0.5 - 2.0 ** -12), scale=0.0625)
-
-        def U(c):
-            tt(W(i + 1, c * CW, c * CW + n * CS), W(i, c * CW, c * CW + n * CS), V(Y[c % 2], 0, n * CS), A.add)
-            send(i + 1, c)
-        did = set()
-
-        def run(text, extra):
-            for w in text.split():
-                if w in extra:
-                    extra[w]()
+    def gathers(i, n, slots):
+        for s in slots:
+            tt(slot("tq", s), IND(win(i), V("ln", 16 * s, 16 * s + 16)), V("rn") if i % 2 == 0 and s == n - 1 else own(i, s), A.subtract)
+            ts(slot("cq", s), slot("tq", s), 256.0, A.min, -256.0, A.max)
+            for c in range(NC):
+                z, d = V("cq", s * P + c * CS, s * P + (c + 1) * CS), V(DB[c], s, CW, S)
+                if c in SCAN[i]:
+                    items = [(d, AM(s, s), z, False, s == n - 1)]
+                elif c and n in WIDE:
+                    d = V(DB[c])
+                    items = ([(V(DB[c], u, CW, S), AM(u, s), z, False, False) for u in range(s, n)]
+                             + ([(d, V("ib"), V("big"), False, False), (d, V("nb"), V("big"), False, False), (d, V("ib"), V("epw"), False, True)] if s == n - 1 else []))
                 else:
-                    {"G": G, "C": C, "F": Fw, "L": FL, "B": B, "U": U}[w[0]](int(w[1]))
-                did.add(w)
-                for c in range(NC):
-                    free = c < 2 or "F%d" % (c - 2) in did
-                    if free and "C%d" % c in did and "P%d" % c not in did:
-                        PE(c)
-                        did.add("P%d" % c)
-                    if ng < n and "P%d" % c in did and "cw" in did and "N%d" % c not in did:
-                        PN(c)
-                        did.add("N%d" % c)
-        return run
+                    items = ([(V(DB[c], u, CW, S), AM(u, s), z, False, False) for u in range(s, n)]
+                             + [(d, V("ib"), V("big", 0, CS), False, False), (d, V("nb"), V("big", 0, CS), False, False),
+                                (d, V("ib"), V("epw", s, CW, S), False, s == n - 1)])
+                for a in range(0, len(items), BATCH):
+                    mms(items[a:a + BATCH])
+                    if s or a:
+                        calls[-1]["after"].add(closing[c])
+                    else:
+                        opening[c] = len(calls) - 1
+                    closing[c] = len(calls) - 1
+            if s == n - 1:
+                turn = sorted(range(NC), key=lambda c: c not in SCAN[i])
+                for c, e in zip(turn, turn[1:]):
+                    in_turn([closing[c], opening[e]])
+    closing, opening = {}, {}
+
+    def result(i, h):
+        half = sl(h * 128, (h + 1) * 128)
+        for s in range(S):
+            act(X("rc", s, half), W(i, along(s, h * 128, (h + 1) * 128)), bias=-M)
+        for k in range(2):
+            dmas("d_yr%d" % (2 * k + h), [("s", D("dyr", sl(2 * k + h, 4 * N, 4)), X("rc", sl(4 * k, 4 * k + 4), half))], 256)
+            ks = []
+            for q in others:
+                piece = D("dyr", 4 * PLACE[q] + 2 * k + h)
+                if (k, h) in RELAYED:
+                    ks.append(hop("h_y%d" % (4 * q + 2 * k + h), piece))
+                else:
+                    ks.append(send(q, X("lyr", 2 * rank + k, half), piece, "a_yr%d" % (4 * rank + 2 * k + h)))
+            for q in others:
+                lands("a_yr%d" % (4 * q + 2 * k + h), [(X("lyr", 2 * q + k, half), q)], ks, 192, 1 + ((k, h) in RELAYED))
+
+    def updates(i, n):
+        last = i == 2 * RO - 1
+        named = min(n if i % 2 else n - 1, S - 1)
+        line = []
+        for c in range(NC):
+            x = XB[c % 2]
+            if c in SCAN[i]:
+                scan(V("d1", 0, CW), V("ta"), V(DB[c]))
+                act(V("d1", CW, 2 * CW), V("d1", 0, CW), bias=M16)
+                act(V(DB[c]), V("d1", CW, 2 * CW), bias=-M16)
+            scan(V(x, 0, CW, -1), V("tc", 0, CW, -1), V(DB[c], 0, CW, -1))
+            line.append(len(calls) - 1)
+            if c in SCAN[i]:
+                act(V(x), V(x), bias=EPS - 0.5)
+            halves = [(0, CW)] if c < NC - 1 else [(0, P), (P, CW)]
+            for h, (a, b) in enumerate(halves):
+                here, there = sl(c * CW + a, c * CW + b), sl(P * S + c * CW + a, P * S + c * CW + b)
+                tt(W(i + 1, here), W(i, here), V(x, a, b), A.add)
+                line.append(len(calls) - 1)
+                if not last:
+                    (move if c == NC - 1 else act)(X("ow", here), W(i + 1, here))
+                if AWAY[c] == "d":
+                    dmas("w%d_%d" % (i, c), [("s", W(i + 1, there, rows(u, k)), W(i + 1, here, rows(v, k))) for u, v, k in moves], 400)
+                elif AWAY[c] == "c":
+                    for u, v, k in moves:
+                        move(W(i + 1, there, rows(u, k)), W(i + 1, here, rows(v, k)))
+                elif c < NC - 1:
+                    mms([(V(DB[c], s, CW, S), V("rot"), W(i + 1, along(s, c * CS, (c + 1) * CS)), True, True) for s in range(named)])
+                    move(W(i + 1, there), V(DB[c]))
+                else:
+                    mms([(V(TURN[h], 0, P), V("rot"), W(i + 1, here), True, True)])
+                    move(W(i + 1, there), V(TURN[h], 0, P))
+            if last and c % 2:
+                result(i + 1, c // 2)
+        in_turn(line)
 
     for r in range(RO):
         f = F0 + r
         n = f + 1
         i = 2 * r
-        run = sweep_parts(i, n, f)
+        m = FIRST[f]
 
-        def gather(k):
-            t = V("td", k * P, (k + 1) * P)
-            tt(t, IND(win(i, True), V("cl", k * 16, (k + 1) * 16)), V("me"), A.subtract)
-            if k < f - 1:
-                act(V(D[k // 2], (k % 2) * P, (k % 2 + 1) * P), t, AF.Abs)
-            if k > 0:
-                act(V("xs", k * P, (k + 1) * P), t, AF.Abs)
+        def dist(k):
+            k -= k >= m
+            return V(DIST[k // 2], (k % 2) * P, (k % 2 + 1) * P)
 
-        def compare(j, k):
-            off = P * (k * (k - 1) // 2 + j)
-            tt(V("lt", off, off + P), V("xs", k * P, (k + 1) * P), V(D[j // 2], (j % 2) * P, (j % 2 + 1) * P), A.is_lt)
+        def first_of(k):
+            return k * (k - 1) // 2 if k < m else m * (m - 1) // 2 + (k - m) * (k - m - 1) // 2
 
-        def counts(k):
-            off = P * (k * (k - 1) // 2)
-            mms([(V(Y[k % 2], 0, 16 * k), EZ(x), V("lt", off + x, off + P * k, 16), x == 0, x == 15) for x in range(16)])
-
-        def beats(k):
-            ts(V3("bb", k, k + 1, 16, 16 * (k + 1)), V(Y[k % 2], 0, 16 * k), 8.5, A.is_lt)
-
-        def step(k):
-            w = 16 * (k + 1)
-            if k == 0:
-                cp(V("pp", 0, w), V3("bb", 0, 1, 0, w))
+        def follow(k):
+            w, a = 16 * (k + 1), 128 * k
+            if k:
+                lo, c1 = P * first_of(k), 128 + 96 * (k % 2)
+                mms([(V(CUR, c1, c1 + 16 * k), EZ(u), V("lt", lo + u, lo + P * k, 16), u == 0, u == 15) for u in range(16)])
+                ts(X("bb", k, sl(16, w)), V(CUR, c1, c1 + 16 * k), 8.5 / 16, A.is_lt)
+                tt(V("pp", a, a + w), V(CUR, 0, w), X("bb", k, sl(0, w)), A.mult)
             else:
-                tt(V("pp", k * 128, k * 128 + w), V(CUR, 0, w), V3("bb", k, k + 1, 0, w), A.mult)
-            mms([(V(CUR, 0, w + 16), V("ih"), V("pp", k * 128, k * 128 + w + 16), True, False)]
-                + [(V(CUR, w, w + 16), V("nh"), V("pp", k * 128 + 16 * j, k * 128 + 16 * j + 16), False, j == k) for j in range(k + 1)])
+                cp(V("pp", a, a + w), X("bb", k, sl(0, w)))
+            mms([(V(CUR, 0, w + 16), V("ib"), V("pp", a, a + w + 16), True, False)]
+                + [(V(CUR, w, w + 16), V("nb"), V("pp", a + 16 * u, a + 16 * u + 16), False, u == k) for u in range(k + 1)])
 
-        def choose(h, table):
-            w = 16 * (f + 1)
-            tt(V("pr", h * 128, h * 128 + w), V(CUR, 0, w), V(table, 0, w), A.mult)
-            mms([(V(D[h], 0, 16), V("ih"), V("pr", h * 128 + 16 * j, h * 128 + 16 * j + 16), j == 0, j == f) for j in range(f + 1)])
+        def choose(out, table, k, x):
+            tt(X("pr", x, sl(0, 16 * k)), V(CUR, 0, 16 * k), table, A.mult)
+            mms([(out, V("ib"), X("pr", x, sl(16 * u, 16 * u + 16)), u == 0, u == k - 1) for u in range(k)])
 
-        preload(n, 0)
-        preload(n, 1)
-        step(0)
-        arrived(i)
-        gather(0)
-        gather(1)
-        gather(2)
-        for k in range(1, f):
-            if k + 2 < f:
-                gather(k + 2)
-            for j in range(k):
-                compare(j, k)
-                if k >= 2 and j == k - 2:
-                    beats(k - 1)
-            if k >= 2:
-                step(k - 1)
-            counts(k)
-        pk = V("pk", 16 * r, 16 * r + 16)
-        oi = V("oi", 16 * r, 16 * r + 16)
-        run(ORDER1, {
-            "beats": lambda: beats(f - 1), "step": lambda: step(f - 1), "cb": lambda: choose(0, "cb"), "cn": lambda: choose(1, "cn"),
-            "pk": lambda: ts(pk, V(D[0], 0, 16), 2048.0 + (f - 1) * CS, A.add),
-            "tn": lambda: tt(V("tn"), IND(win(i), pk), V("rn"), A.subtract),
-            "cw": lambda: ts(V("cw"), V("tn"), 256.0, A.min, -256.0, A.max),
-            "oi": lambda: ts(oi, V(D[1], 0, 16), 2048.0 + (f - 1) * P, A.add)})
-        preload(n, 0)
-        preload(n, 1)
-        own_copy(i + 1, n)
         for c in range(NC):
-            cp(V("lst", c * 32 + 4 * f, c * 32 + 4 * f + 4), V("pk", 16 * r + 4 * c, 16 * r + 4 * c + 4))
-        cp(V("yos", 16 * r, 16 * r + 16), oi)
-        if r == 0:
-            dmas("l_l5", [("s", T.lrep5[x::16, 8:], T.oi[:, 0:16], [oi], [V("lrep5", 8)] if x == 0 else []) for x in range(16)])
-        if r < RO - 1:
-            tables(n + 1)
-            table_list(oi, 16, 80 if r == 0 else 16, 64 if r == 0 else 0)
-            gen = candidates(16, "lrep" if r == 0 else "lrep5", V("ci", 0, 16), D[2])
-            next(gen)
-            next(gen, None)
-            describe(16, 0, f)
+            preload(i, c)
+        for k in range(f):
+            tt(slot("td", k), IND(win(i), V("cl", k * 16, (k + 1) * 16)), own(i, f - 1), A.subtract)
+            if k != m - 1:
+                act(dist(k), slot("td", k), AF.Abs)
+            if (k > 0 or m < f) and k != m:
+                act(slot("xs", k), slot("td", k), AF.Abs)
+        for k in range(f):
+            for j in range(0 if k < m else m, k):
+                tt(slot("lt", first_of(k) + j - m * (k >= m)), slot("xs", k), dist(j), A.is_lt)
+        gathers(i, n, range(f))
+        for k in range(m):
+            follow(k)
+        best, place = V(CUR, 320, 336), V(CUR, 336, 352)
+        if m < f:
+            choose(place, V("ix", 0, 16 * (m + 1)), m + 1, 0)
+            choose(best, V("cb", 0, 16 * (m + 1)), m + 1, 1)
+            ts(V("gi"), place, 0.0, A.add)
+            cp(V("da"), IND(V("xs"), V("gi")))
+            a0, a1, a2 = (V("cb", 16 * (k + 1), 16 * (k + 2)) for k in range(m, f))
+            lo = P * first_of(m)
+            mms([(V(CUR, 352, 400), EZ(u), V("lt", lo + u, lo + 3 * P, 16), u == 0, u == 15) for u in range(16)])
+            ts(X("hw", 0), V(CUR, 352, 368), 8.5 / 16, A.is_lt, -1.0, A.mult)
+            ts(X("hw", sl(1, 3)), V(CUR, 368, 400), 8.5 / 16, A.is_lt)
+            tt(X("hw", 3), a2, a1, A.subtract)
+            tt(X("hw", 4), a0, a2, A.subtract)
+            tt(X("hz", 1, sl(1, 64, 4)), X("hw", 2), X("hw", 3), A.mult)
+            tt(X("hw", 5), X("hw", 1), X("hw", 4), A.mult)
+            tt(X("hw", 6), X("hw", 5), X("hz", 1, sl(1, 64, 4)), A.add)
+            tt(X("hz", 1, sl(2, 64, 4)), X("hw", 0), X("hw", 6), A.mult)
+            tt(X("hw", 7), a2, X("hz", 1, sl(1, 64, 4)), A.subtract)
+            tt(X("hz", 1, sl(3, 64, 4)), X("hw", 7), X("hz", 1, sl(2, 64, 4)), A.subtract)
+            tt(X("hz", 1, sl(0, 64, 4)), best, a2, A.subtract)
+            for k in range(m, f):
+                tt(X("l4", sl(f - k, 64, 4)), V("da"), dist(k), A.is_gt)
+            mms([(V(CUR, 400, 464), EZ(u), X("l4", sl(None), u), u == 0, u == 15) for u in range(16)])
+            ts(X("hz", 0), V(CUR, 400, 464), 8.5 / 16, A.is_lt)
+            scan(X("hz", 2), X("hz", 0), X("hz", 1))
+            best = X("hz", 2, sl(3, 64, 4))
         else:
-            ts(V("i32"), col, row, A.is_equal)
-            dmas("l_out", [("s", T.yo[:], T.yos[:], [V("yos")], [])])
-
-        arrived(i + 1)
-        sweep_parts(i + 1, n, n)(ORDER2, {})
+            choose(best, V("cb", 0, 16 * (f + 1)), f + 1, 2)
+        half = V(DIST[2 * (m == f)], 0, P)
+        mms([(half, V("sh"), X("mer", r), True, False), (half, V("sh2"), X("mn", r), False, False), (half, V("ib"), V("qrt"), False, True)])
+        act(V("rn"), half, bias=M)
+        ts(V("ln", 16 * f, 16 * f + 16), best, f - 1.0, A.add)
+        ts(V("lh", 16 * f, 16 * f + 16), best, f - 1.0 - 2048, A.add)
+        act(V("yo2", 16 * r, 16 * r + 16), best, scale=0.125, bias=float(P * (f - 1)))
         if r < RO - 1:
-            for c in range(NC):
-                newest(i + 2, n, c)
-            for _ in new_rating(i + 2, n):
-                pass
-        own_copy(i + 2, n)
-    for c in range(NC):
-        act(V3("yrs", 0, 8, c * CS, (c + 1) * CS), W(6, c * CW, (c + 1) * CW), bias=-M)
+            ts(V("gl", 0, 16), best, 0.125, A.mult, float(P), A.min)
+            ts(V("oa", 0, 16), V("lh", 16 * f, 16 * f + 16), 0.0, A.max)
+        gathers(i, n, [f])
+        act(W(i, along(f)), V("rn"))
+        updates(i, n)
 
-    dmas("l_out", [("s", T.yr[:], T.yrs[:], [V3("yrs", 0, 8, 0, 256)], [])])
-    arrived(6)
-
-    def GF(c):
-        t = V("d1", c * CW, (c + 1) * CW)
-        tt(t, IND(win(6), V("lst", c * 32, (c + 1) * 32)), V("rc", c * CW, (c + 1) * CW), A.subtract)
-        act(V("ps%d" % c), t, AF.Sigmoid, scale=-1.0 / 256)
-
-    def MF(c):
-        a = c * CW
-        if c < NC - 1:
-            tt(V("d3", a, a + CW), V("ps%d" % c), V3("sts", 0, 8, c * CS, (c + 1) * CS), A.mult)
-            mms([(V("ps%d" % (4 + c), 0, CS), V("i32"), V("d3", a + s * CS, a + (s + 1) * CS), s == 0, s == S - 1) for s in range(S)])
+        if r == 0 and any(SCAN):
+            c = max(max(x, default=0) for x in SCAN)
+            ts(V("muf", 57, 64), V("muf", 0, 7), -K0, A.mult, K0, A.add)
+            for s in range(S):
+                act(V("og", s, CW, S), V("ocs", s * P + c * CS, s * P + (c + 1) * CS), scale=0.0625, bias=mu(56 + s) if s else K0)
+        for c in range(NC):
+            preload(i + 1, c)
+        if r < RO - 1:
+            mms([(V(CUR, u, P, 16), X("bi", u), V("lh", 16 * (f - 1), 16 * f), True, True) for u in range(16)])
+            act(V("tb", 0, P), V(CUR, 0, P))
+            candidates(16, f, "tb", CUR)
+            factors(n, "a")
+            act(X("do", along(f)), X("do", along(f)), bias=mu(24 + f))
         else:
-            tt(V("d3", a, a + 256), V("ps%d" % c, 0, 256), V3("sts", 0, 4, c * CS, (c + 1) * CS), A.mult)
-            tt(V(CUR, 0, 256), V("ps%d" % c, 256, 512), V3("sts", 4, 8, c * CS, (c + 1) * CS), A.mult)
-            tt(V("d3", a + 256, a + 384), V(CUR, 0, 128), V("d3", a, a + 128), A.add)
-            tt(V(CUR, 256, 384), V(CUR, 128, 256), V("d3", a + 128, a + 256), A.add)
-            tt(V("d3", a + 384, a + 448), V(CUR, 256, 320), V("d3", a + 256, a + 320), A.add)
-            tt(V(CUR, 384, 448), V(CUR, 320, 384), V("d3", a + 320, a + 384), A.add)
-            tt(V("ys", c * CS, (c + 1) * CS), V(CUR, 384, 448), V("d3", a + 384, a + 448), A.add)
-    GF(0)
-    GF(1)
-    GF(2)
-    MF(0)
-    MF(1)
-    GF(3)
-    MF(2)
-    for c in range(NC - 1):
-        act(V("ys", c * CS, (c + 1) * CS), V("ps%d" % (4 + c), 0, CS))
-    MF(3)
-    dmas("l_out", [("a", T.y[:], T.ys[:], [V("ys")], [])])
-    for s_, c_ in count.items():
-        wait("g", (s_, c_))
+            ts(V("yo1"), V("lh", 80, 128), 0.0, A.is_ge, 1792.0, A.mult)
+            tt(V("yos"), V("yo1"), V("yo2"), A.add)
+            dmas("d_yo", [("s", D("dyo", sl(None)), V("yos"))], 24)
+            lands("a_yo", [(X("lyo", q), q) for q in others], [send(q, X("lyo", rank), D("dyo", PLACE[q]), "a_yo") for q in others], 100)
+            dmas("out", [("s", T.yo[rows(q), :], X("lyo", q)) for q in others] + [("s", T.yo[rows(rank), :], X("yos", parts=rows(PLACE[rank])))], 24)
+        gathers(i + 1, n, range(n))
+        updates(i + 1, n)
+        if r < RO - 1:
+            tables(f)
+            newest(r + 1, W(i + 2, along(f)), -M)
+
+    dmas("out", [("s", T.yr[rows(rank), :], X("rc", parts=rows(PLACE[rank])))], 500)
+    for k in range(2):
+        for q in others:
+            dmas("out", [("s", T.yr[rows(q), 1024 * k:1024 * (k + 1)], X("lyr", 2 * q + k))], 128)
+
+    for k in range(4):
+        for s in (2 * k, 2 * k + 1):
+            tt(slot("d1", s), IND(win(2 * RO), V("ln", 16 * s, 16 * s + 16)), X("rc", s), A.subtract)
+        act(V(DB[k]), slot("d1", 2 * k, 2 * k + 2), AF.Sigmoid, scale=-1.0 / 256, bias=M / 256, more=0 if k else 1300)
+        if k:
+            calls[-1]["after"].add(closing[0])
+        closing[0] = len(calls) - 1
+    for k in range(2):
+        tt(slot("d3", 2 * k, 2 * k + 2), V(DB[k]), slot("sts", 2 * k, 2 * k + 2), A.mult)
+        mms([(V(TURN[0], 0, P), V("i32"), slot("d3", s), s == 0, s == 3) for s in (2 * k, 2 * k + 1)])
+    tt(slot("d3", 4, 6), V(DB[2]), slot("sts", 4, 6), A.mult)
+    tt(V(CUR), V(DB[3]), slot("sts", 6, 8), A.mult)
+    tt(slot("d3", 6), V(CUR, 0, P), slot("d3", 4), A.add)
+    tt(V(XB[0], 0, P), V(CUR, P, 2 * P), slot("d3", 5), A.add)
+    tt(slot("d3", 7), V(TURN[0], 0, P), slot("d3", 6), A.add)
+    tt(V("ys"), V(XB[0], 0, P), slot("d3", 7), A.add)
+    ks = []
+    for k, q in enumerate(others):
+        a = 128 * PLACE[q] + 4
+        mms([(V(DB[k], 0, CS), V("zq", a - c, a + 128 - c), V("ys", c * CS, (c + 1) * CS), c == 0, c == 3) for c in range(4)])
+        cp(X("sy", q), V(DB[k], 0, CS))
+        ks.append(send(q, X("ly", rank), X("sy", q), "a_y%d" % rank))
+    dmas("out", [("a", T.y[rows(rank), :], X("ys", parts=rows(PLACE[rank])))], 32)
+    for k, q in zip(reversed(ks), others):
+        lands("a_y%d" % q, [(X("ly", q), q)], [k], 32)
+        dmas("out", [("a", T.y[rows(q), :], X("ly", q))], 32)
+    issue(calls, Q, T)

import numpy as np
from concourse.bass import DstId, RemoteDMATransfer
from concourse.mybir import AluOpType, ActivationFunctionType

P, S, F0, RO, N = 256, 8, 5, 3, 4
NC, CS = 4, 64
CW = CS * S
FAR = 2 * P * S
M = 12582912.0
M16 = M / 16
K0 = (-0.5 + 2.0 ** -8) / 16
EPS = 2.0 ** -12
H16, B16, F32 = "float16", "bfloat16", "float32"
PLACE = [0, 2, 1, 3]
FIRST = {5: 5, 6: 3, 7: 4}
RELAYED = [(0, 0), (0, 1)]
AWAY = "ddpc"
CYCLE, GATHER, PE_CYCLE, HOP, DMA_START, WRITE_START = 0.83, 1.4, 0.42, 100, 1500, 1800
BATCH = 5
WIDE = (8,)
SCAN = [(), (), (), (2,), (), (2,)]

SCRATCH = {}
for _i in range(2):
    SCRATCH["W%d" % _i] = ("sbuf", [128, FAR + S], F32)
for _i in range(8):
    SCRATCH["ps%d" % _i] = ("psum", [128, 512], F32)
SCRATCH.update({
    "ops": ("sbuf", [128, 80], "int32"), "mus": ("sbuf", [128, 16], B16), "lp": ("sbuf", [128, N, 96], H16),
    "s32": ("sbuf", [128, N, 320], "int32"), "s16": ("sbuf", [128, N, 320], H16),
    "so": ("sbuf", [128, N, 512], B16), "ss": ("sbuf", [128, N, 512], B16),
    "dr": ("dram", [N, 128, 320], H16), "dc": ("dram", [N, 128, 512], B16), "ds": ("dram", [N, 128, 512], B16),
    "r16": ("sbuf", [128, 1280], H16), "ocs": ("sbuf", [128, 2048], B16), "sts": ("sbuf", [128, 2048], B16),
    "dyr": ("dram", [4 * N, 128, 128], F32), "lyr": ("sbuf", [128, 2 * N, 256], F32),
    "sy": ("sbuf", [128, N, 64], F32), "ly": ("sbuf", [128, N, 64], F32), "zq": ("sbuf", [128, 516], F32),
    "dyo": ("dram", [N, 128, 12], F32), "lyo": ("sbuf", [128, N, 12], F32),
    "yos": ("sbuf", [128, 48], F32), "yo1": ("sbuf", [128, 48], F32), "yo2": ("sbuf", [128, 48], F32), "ys": ("sbuf", [128, 256], F32),
    "colx": ("sbuf", [128, 224], F32), "colg": ("sbuf", [128, 128], F32), "rowi": ("sbuf", [128, 8], "int32"),
    "rowf": ("sbuf", [128, 8], F32), "rowg": ("sbuf", [128, 8], F32), "ones": ("sbuf", [128, 516], B16),
    "pt0": ("sbuf", [128, 80], F32), "ptab": ("sbuf", [128, 80], F32), "mk": ("sbuf", [128, 16], F32),
    "ib": ("sbuf", [128, 128], B16), "nb": ("sbuf", [128, 128], B16), "i32": ("sbuf", [128, 128], F32),
    "rot": ("sbuf", [128, 128], F32), "rot16": ("sbuf", [128, 128], B16), "sh": ("sbuf", [128, 128], F32), "sh2": ("sbuf", [128, 128], F32),
    "t0": ("sbuf", [128, 128], F32), "t1": ("sbuf", [128, 128], F32), "t2": ("sbuf", [128, 128], F32),
    "ez": ("sbuf", [128, 144], B16), "sel": ("sbuf", [128, 224], B16), "bo": ("sbuf", [128, 128], B16), "bi": ("sbuf", [128, 16, 128], B16),
    "am": ("sbuf", [128, 29, 128], B16), "big": ("sbuf", [128, CW], B16), "qrt": ("sbuf", [128, P], B16),
    "epw": ("sbuf", [128, CW], B16), "tc": ("sbuf", [128, CW], F32),
    "ta": ("sbuf", [128, CW], F32), "og": ("sbuf", [128, CW], F32),
    "l4": ("sbuf", [128, 64, 16], B16), "hz": ("sbuf", [128, 3, 64], F32), "hw": ("sbuf", [128, 8, 16], F32),
    "muf": ("sbuf", [128, 64], F32), "ix": ("sbuf", [128, 96], H16), "ix0": ("sbuf", [128, 80], F32),
    "xa": ("sbuf", [128, 80], "int32"), "xb": ("sbuf", [128, 80], "int32"), "xc": ("sbuf", [128, 80], "int32"), "xo": ("sbuf", [128, 80], "int32"),
    "xd": ("sbuf", [128, 80], F32), "xe": ("sbuf", [128, 80], F32), "xf": ("sbuf", [128, 80], F32), "xg": ("sbuf", [128, 80], F32),
    "xh": ("sbuf", [128, 80], F32), "hm": ("sbuf", [128, 80], F32), "co": ("sbuf", [128, 80], "int32"), "a8": ("sbuf", [128, 80], "int32"),
    "a0": ("sbuf", [128, 16], "int32"),
    "lh": ("sbuf", [128, 128], H16), "oa": ("sbuf", [128, 80], H16), "lrep": ("sbuf", [128, 1288], F32), "tb": ("sbuf", [128, 264], F32),
    "gl": ("sbuf", [128, 80], "uint16"), "ln": ("sbuf", [128, 128], "uint16"), "cl": ("sbuf", [128, 112], "uint16"), "gi": ("sbuf", [128, 16], "uint16"),
    "cb": ("sbuf", [128, 128], H16), "bb": ("sbuf", [128, 8, 128], H16), "pp": ("sbuf", [128, 7 * 128], H16), "pr": ("sbuf", [128, 3, 128], H16),
    "mer": ("sbuf", [128, RO, P], F32), "mn": ("sbuf", [128, RO, P], F32), "rn": ("sbuf", [128, P], F32), "da": ("sbuf", [128, P], F32),
    "td": ("sbuf", [128, 1792], F32), "xs": ("sbuf", [128, 1800], F32), "lt": ("sbuf", [128, 21 * 256], H16), "lc": ("sbuf", [128, 1280], H16),
    "tq": ("sbuf", [128, 2048], B16), "cq": ("sbuf", [128, 2048], B16),
    "do": ("sbuf", [128, P * S], F32), "rc": ("sbuf", [128, S, P], F32), "ow": ("sbuf", [128, 2048], F32),
    "d1": ("sbuf", [128, 2048], F32), "d3": ("sbuf", [128, 2048], F32),
})
SEMAPHORES = (["cv", "ca", "cp", "cg", "sent", "l_op", "l_mu", "l_ss", "l_dr", "l_dc", "l_ds", "l_r", "l_oc", "l_st",
               "a_lp", "a_r", "a_c", "a_s", "a_yo", "d_yo", "out"]
              + ["h_c%d" % j for j in range(N)] + ["h_s%d" % j for j in range(N)] + ["h_y%d" % j for j in range(4 * N)]
              + ["l_s%d" % j for j in range(N)] + ["l_o%d" % j for j in range(N)] + ["a_mn%d" % r for r in range(RO)]
              + ["a_y%d" % j for j in range(N)] + ["d_yr%d" % k for k in range(4)] + ["a_yr%d" % k for k in range(4 * N)]
              + ["w%d_%d" % (i, c) for i in range(6) for c in range(NC)])


def bits(mask):
    return bin(mask).count("1")


def helpers_of(src, topo, T):
    return [h for h in topo.cores_of(src)
            if topo.die(h) != topo.die(src) and T.rank_of(h) is None and all(topo.may_write(h, c) for c in T.cores)]


def relayed(T, rank, topo):
    others = [(rank + k) % N for k in range(1, N)]
    hs = helpers_of(T.cores[rank], topo, T)
    jobs = ([(T.so[:, q], "h_c%d" % q, q, T.dc[PLACE[rank]], "a_c") for q in others[1:]]
            + [(T.ss[:, q], "h_s%d" % q, q, T.ds[PLACE[rank]], "a_s") for q in others]
            + [(T.lyr[:, 2 * q + k, 128 * h:128 * h + 128], "h_y%d" % (4 * q + 2 * k + h), q,
                T.lyr[:, 2 * rank + k, 128 * h:128 * h + 128], "a_yr%d" % (4 * rank + 2 * k + h)) for k, h in RELAYED for q in others])
    return [(hs[k % len(hs)],) + job for k, job in enumerate(jobs)]


def hop_mask(src, topo, T):
    return topo.mask(src, helpers_of(src, topo, T)[0]) & ~topo.mask(src, [c for c in T.cores if c != src][0])


def helper_program(g, core, rank, T, topo):
    total = 0
    for h, here, sem, q, there, sem_there in relayed(T, rank, topo):
        if h != core:
            continue
        rid, pid, _ = topo.addr(T.cores[q])
        mask = topo.mask(core, T.cores[q])
        g.wait_ge(T.sem[sem], bits(hop_mask(T.cores[rank], topo, T)))
        g.remote_dma(there, here, T.sem[sem_there], T.sem["sent"], pid, rid, mask)
        total += bits(mask)
    g.wait_ge(T.sem["sent"], total)


def issue(calls, Q, T):
    for k, c in enumerate(calls):
        c["next"] = []
        for j in c["after"]:
            calls[j]["next"].append(k)
    todo = list(range(len(calls)))
    while todo:
        c = calls[todo[-1]]
        open_ = [k for k in c["next"] + c["then"] if "way" not in calls[k]]
        if open_:
            todo += open_
            continue
        c["way"] = max([c["lat"] + calls[k]["way"] + HOP for k in c["next"]] + [c["busy"] + calls[k]["way"] for k in c["then"]], default=c["lat"])
        c["left"], c["from"] = len(c["after"]), 0.0
        todo.pop()
    free = {q: 0.0 for q in list(Q) + ["x"]}
    bank = {}
    ready = [k for k, c in enumerate(calls) if not c["left"]]
    line = []

    def start(k, q):
        c = calls[k]
        t = max(free[q], c["from"])
        for b in c["banks"]:
            for x, j in bank.get(b, {}).items():
                if x != q:
                    t = max(t, calls[j]["end"] + HOP)
        return t
    while ready:
        when = {(k, q): start(k, q) for k in ready for q in calls[k]["q"]}
        k, q = min(when, key=lambda x: (when[x], x[1]))
        k = max((j for j, x in when if x == q and when[j, q] <= when[k, q] + HOP / 2), key=lambda j: (calls[j].get("first", -99), calls[j]["way"], -j))
        c = calls[k]
        if len(c["q"]) > 1:
            c["emit"], c["q"] = c["emit"][q], q
        ready.remove(k)
        for b in c["banks"]:
            c["waits"] |= set(j for x, j in bank.setdefault(b, {}).items() if x != q)
            bank[b][q] = k
        c["end"] = when[k, q] + c["lat"]
        if q != "x":
            free[q] = when[k, q] + c["busy"]
        line.append(k)
        for j in c["next"]:
            d = calls[j]
            d["from"] = max(d["from"], c["end"] + (0 if q == d["q"] == "p" else HOP))
            d["left"] -= 1
            if not d["left"]:
                ready.append(j)
    needed = set(j for c in calls for j in c["waits"])
    count, seen = {}, {q: {} for q in Q}

    def wait(q, sem, n):
        if seen[q].get(sem, 0) < n:
            Q[q].wait_ge(T.sem[sem], int(n))
            seen[q][sem] = n
    for k in line:
        c = calls[k]
        if c["q"] != "x":
            need = {}
            for j in c["waits"]:
                sem, n = calls[j]["token"]
                need[sem] = max(need.get(sem, 0), n)
            for sem, n in need.items():
                wait(c["q"], sem, n)
            ins = c["emit"]()
            if "token" not in c:
                sem = "c" + c["q"]
                if k in needed:
                    ins.then_inc(T.sem[sem], 1)
                    count[sem] = count.get(sem, 0) + 1
                c["token"] = (sem, count.get(sem, 0))
        count[c["token"][0]] = max(count.get(c["token"][0], 0), c["token"][1])
    for sem, n in count.items():
        wait("g", sem, n)


def rank_program(g, core, T, topo):
    cores = list(T.cores)
    rank = T.rank_of(core)
    if rank is None:
        for r in range(N):
            if core in helpers_of(cores[r], topo, T):
                helper_program(g, core, r, T, topo)
        return
    others = [(rank + k) % N for k in range(1, N)]
    A = AluOpType
    AF = ActivationFunctionType
    calls, total = [], {}
    writer, readers, grid = {}, {}, {}
    sl = slice

    def cells(name):
        if name not in grid:
            where, shape, _ = SCRATCH[name]
            grid[name] = np.arange(shape[0]) if where == "dram" else np.arange(int(np.prod(shape[1:]))).reshape(shape[1:])
            writer[name] = np.full((4, grid[name].size), -1)
            readers[name] = []
        return grid[name]

    def X(name, *ix, parts=sl(0, 128)):
        return (T[name][(parts,) + ix], name, np.ravel(cells(name)[ix]), sl(parts.start // 32, parts.stop // 32))

    def V(name, a=0, b=None, step=1):
        if b is None:
            b = cells(name).size
        if step > 0:
            return X(name, sl(a, b, step) if step > 1 else sl(a, b))
        return (T[name][:, b - 1:(a - 1 if a else None):-1], name, cells(name)[a:b], sl(0, 4))

    def D(name, ix):
        return (T[name][ix], name, np.ravel(cells(name)[ix]), sl(0, 4))

    def IND(win, off):
        return (win[0].indirect(off[0]),) + win[1:] + (off,)

    def note(q, emit, busy, reads, writes, lat=None, token=None, after=()):
        k = len(calls)
        deps, waits = set(after), set()
        reads = [x for r in reads for x in ([r] if len(r) == 4 else [r[:4], r[4]])]
        for v, is_w in [(r, False) for r in reads] + [(w, True) for w in writes]:
            _, name, cols, parts = v
            found = [int(j) for j in np.unique(writer[name][parts, cols]) if j >= 0]
            if is_w:
                mark = np.zeros(writer[name].shape, bool)
                mark[parts, cols] = True
                found += [j for j, p_, c_ in readers[name] if mark[p_, c_].any()]
                readers[name] = [x for x in readers[name] if not mark[x[1], x[2]].all()]
            for j in found:
                for x in calls[j]["mates"]:
                    deps.add(x)
                    if calls[x]["q"] != q or q in "ava" or (q != "p" and not is_w):
                        waits.add(x)
        for _, name, cols, parts in reads:
            readers[name].append((k, parts, cols))
        for _, name, cols, parts in writes:
            writer[name][parts, cols] = k
        c = {"q": q, "emit": emit, "busy": busy, "lat": busy if lat is None else lat, "after": deps - {k}, "waits": waits - {k}, "mates": [k], "then": [],
             "banks": set(v[1] for v in reads + list(writes) if v[1][:2] == "ps")}
        if token:
            c["token"] = token
        calls.append(c)
        return k

    def sc(x):
        return x if isinstance(x, (int, float)) or x is None else x[0]

    def aps(*xs):
        return [x for x in xs if isinstance(x, tuple)]

    def kind(v):
        return SCRATCH[v[1]][2]

    def cost(fixed, out, ins, two=False):
        n = len(out[2])
        if any(len(x) == 5 for x in ins):
            return 50 + fixed + n * GATHER * CYCLE
        k = 2 if two and all(x[1][:2] != "ps" for x in ins) else 1
        if all(kind(x) in (H16, B16, "uint16") for x in [out] + ins):
            k /= 2
        return fixed + max(64, n * k) * CYCLE

    def ts(out, in0, s1, op0, s2=None, op1=None):
        args = (out[0], in0[0], sc(s1), sc(s2), op0) + (() if op1 is None else (op1,))
        note("v", lambda: g.vector.tensor_scalar(*args), cost(15, out, [in0]), aps(in0, s1, s2), [out])

    def tt(out, in0, in1, op):
        note("v", lambda: g.vector.tensor_tensor(out[0], in0[0], in1[0], op), cost(15, out, [in0, in1], True), [in0, in1], [out])

    def cp(out, in_):
        note("v", lambda: g.vector.tensor_copy(out[0], in_[0]), cost(15, out, [in_]), [in_], [out])

    def fill(out, x):
        note("v", lambda: g.vector.memset(out[0], x), cost(15, out, []), [], [out])

    def scan(out, d0, d1):
        note("v", lambda: g.vector.tensor_tensor_scan(out[0], d0[0], d1[0], 0.0, A.mult, A.add), cost(15, out, [d1]), [d0, d1], [out])

    def act(out, in_, func=AF.Identity, bias=0.0, scale=1.0, more=0):
        note("a", lambda: g.scalar.activation(out[0], in_[0], func, bias=sc(bias), scale=sc(scale)),
             30 + more + max(64, len(out[2])) * CYCLE, aps(in_, bias, scale), [out])

    def move(out, in_, bias=0.0):
        note("av", {"a": lambda: g.scalar.activation(out[0], in_[0], AF.Identity, bias=bias, scale=1.0),
                    "v": lambda: g.vector.tensor_scalar(out[0], in_[0], bias, None, A.add)}, 25 + max(64, len(out[2])) * CYCLE, [in_], [out])

    def in_turn(ks):
        for j, k in zip(ks, ks[1:]):
            calls[j]["then"].append(k)

    def mms(items):
        def emit():
            for out, lt_, rhs, st, sp in items:
                ins = g.tensor.matmul(out[0], lt_[0], rhs[0], st, sp)
            return ins
        note("p", emit, sum(8 + max(64, len(x[2][2])) * PE_CYCLE * (4 if kind(x[1]) == F32 else 1) for x in items),
             [v for x in items for v in x[1:3]], [x[0] for x in items])

    def iota(out, pattern, mult):
        more = {} if kind(out) == "int32" else {"allow_small_or_imprecise_dtypes": True}
        note("g", lambda: g.iota(out[0], pattern, 0, mult, **more), 130 + 2 * len(out[2]) * CYCLE, [], [out])

    def dmas(sem, items, kib, after=()):
        total[sem] = total.get(sem, 0) + 16 * len(items)
        first = len(calls)
        for q, o, i_ in items:
            def emit(q=q, o=o, i_=i_):
                Q[q].dma_start(o[0] if isinstance(o, tuple) else o, i_[0] if isinstance(i_, tuple) else i_).then_inc(T.sem[sem], 16)
            note(q, emit, 60, aps(i_), aps(o), DMA_START + 3 * kib, (sem, total[sem]), after)
        for k in range(first, len(calls)):
            calls[k]["mates"] = list(range(first, len(calls)))
        return len(calls) - 1

    def remote(to, out, in_, sem, mask):
        rid, pid, _ = topo.addr(to)
        total["sent"] = total.get("sent", 0) + bits(mask)
        return note("g", lambda: g.remote_dma(out, in_[0], T.sem[sem], T.sem["sent"], pid, rid, mask), 250, [in_], [], token=("sent", total["sent"]))

    def send(q, out, in_, sem):
        return remote(cores[q], out[0], in_, sem, topo.mask(core, cores[q]))

    def hop(sem, in_):
        h, there = [x[:2] for x in relayed(T, rank, topo) if x[2] == sem][0]
        return remote(h, there, in_, sem, hop_mask(core, topo, T))

    def lands(sem, places, after, kib, hops=1):
        n = sum(bits(topo.mask(cores[q], core)) for _, q in places)
        note("x", None, 0, [], [v for v, _ in places], hops * WRITE_START + 10 * kib, (sem, n), after)

    Q = {"v": g.vector, "a": g.scalar, "p": g.tensor, "g": g, "s": g.sync}

    def rows(j, k=1):
        return sl(32 * j, 32 * (j + k))

    def W(i, ix, parts=sl(0, 128)):
        return X("W%d" % (i % 2), ix, parts=parts)

    def win(i):
        return V("W%d" % (i % 2))

    def chunk(c, away=0):
        return sl(away * P * S + c * CW, away * P * S + (c + 1) * CW)

    def along(s, a=0, b=P):
        return sl(a * S + s, b * S, S)

    def slot(name, a, b=None):
        return V(name, a * P, (a + 1 if b is None else b) * P)

    def own(i, s):
        return X("rc", s) if i == 0 else X("ow", along(s))

    def mu(k):
        return V("muf", k, k + 1)

    moves = []
    for x in range(N):
        y = PLACE[(PLACE.index(x) + 1) % N]
        if moves and moves[-1][0] % 2 == moves[-1][1] % 2 == 0 and moves[-1][2] == 1 and y == moves[-1][1] + 1:
            moves[-1][2] = 2
        else:
            moves.append([x, y, 1])
    DB, XB, DIST, CUR, TURN = ("ps0", "ps1", "ps2", "ps3"), ("ps4", "ps5"), ("ps4", "ps5", "ps6"), "ps7", ("ps6", "ps7")

    dmas("l_op", [("s", V("ops"), T.opp[:])], 40)
    dmas("l_mu", [("a", V("mus", 0, 14), T.mu[:])], 40)
    for k, j in enumerate(others + [rank]):
        dmas("l_s%d" % j, [("sa"[k % 2], X("s32", j), T.r0[rows(j), :])], 200 * (k + 2))
    for k, j in enumerate(others[1:] + others[:1]):
        dmas("l_o%d" % j, [("sa"[k % 2], X("so", j), T.oc[rows(j), :])], 1000 + 128 * (k + 1))
    dmas("l_dc", [("a", D("dc", PLACE[rank]), T.oc[rows(rank), :])], 128)
    for k, c in enumerate(calls):
        c["first"] = -k

    iota(V("rowi", 0, 1), [[0, 1]], 1)
    iota(V("colx"), [[1, 224]], 0)
    iota(V("colg"), [[16, 8], [0, 16]], 0)
    iota(V("pt0"), [[0, 5], [128, 16]], 0)
    iota(V("ix0"), [[256, 5], [16, 16]], 0)
    row, col, one = V("rowf", 0, 1), V("colx", 0, 128), V("ones", 0, CS)
    fill(X("lp", rank, sl(88, 96)), 0.0)
    fill(V("pp"), 1.0)
    fill(V("ones"), 1.0)
    for k, x in enumerate((112, 15, 16, 96)):
        ts(V("rowi", k + 1, k + 2), V("rowi", 0, 1), x, A.bitwise_and)
    cp(V("rowf", 0, 5), V("rowi", 0, 5))
    ts(V("rowf", 5, 6), V("rowf", 4, 5), 32.0 * rank, A.not_equal, 1000.0, A.mult)
    ts(V("rowf", 6, 7), V("rowf", 5, 6), row, A.add, 96.0 - 32 * rank, A.add)
    ts(V("sel"), V("colx"), V("rowf", 6, 7), A.is_equal)
    ts(V("ib"), col, row, A.is_equal)
    ts(V("bo"), V("colg"), V("rowf", 1, 2), A.is_equal)
    ts(V("mk"), V("colx", 0, 16), V("rowf", 2, 3), A.is_equal)
    for i in range(16):
        act(X("bi", i), V("bo"), scale=V("mk", i, i + 1))
    act(V("nb"), V("ib"), scale=-1.0)
    act(X("am", 0), V("ib"), scale=0.0625)
    act(V("i32"), V("ib"))
    for s in range(F0 + 1, S):
        act(W(0, along(s)), V("ones", 0, P), scale=M)
    for s in range(F0, S):
        act(V("tc", s, CW, S), one, scale=0.0)
    ts(V("rowg", 0, 1), V("rowf", 1, 2), 15.0, A.add)
    ts(V("rowg", 1, 2), V("rowf", 2, 3), 8.0, A.mult)
    ts(V("rowg", 2, 3), V("rowf", 3, 4), 1.0 / 32, A.mult)
    ts(V("rowg", 3, 4), V("rowf", 3, 4), -1.0 / 32, A.mult, 0.5, A.add)
    for x, y, k in moves:
        ts(X("rowg", sl(4, 5), parts=rows(y, k)), X("rowf", sl(0, 1), parts=rows(y, k)), 32.0 * (x - y), A.add)
    ts(V("t0"), col, row, A.subtract)
    ts(V("ez"), V("colx", 0, 144), V("rowg", 0, 1), A.is_equal, 0.0625, A.mult)
    ts(V("ptab"), V("pt0"), V("rowg", 1, 2), A.add)
    ts(V("ix", 16, 96), V("ix0"), V("rowf", 2, 3), A.add)
    fill(V("ix", 0, 16), 1792.0)
    fill(V("xs", 1792, 1800), 131072.0)
    act(X("l4", sl(0, 64, 4)), V("ones", 0, P))
    fill(V("lrep", 0, 8), 0.0)
    fill(V("tb", P, P + 8), 0.0)
    act(V("big"), V("ones", 0, CW), scale=M16)
    act(V("qrt"), V("ones", 0, P), scale=-0.25)
    act(V("epw"), V("ones", 0, CW), scale=EPS)
    for i in range(2):
        fill(W(i, sl(FAR, FAR + S)), M + 262144.0)
    ts(V("t1"), V("t0"), -16.0, A.is_equal, V("rowg", 2, 3), A.mult)
    ts(V("t2"), V("t0"), 0.0, A.is_equal, 0.5, A.mult)
    tt(V("sh"), V("t1"), V("t2"), A.add)
    ts(V("sh2"), V("t0"), 16.0, A.is_equal, V("rowg", 3, 4), A.mult)
    ts(V("rot"), col, V("rowg", 4, 5), A.is_equal)
    act(V("rot16"), V("rot"))

    o = V("ops")
    ts(V("xa"), o, 255, A.bitwise_and)
    ts(V("xc"), o, 2303, A.bitwise_and)
    ts(V("xb"), o, 8, A.arith_shift_right, 7, A.bitwise_and)
    ts(V("xd"), V("xa"), 7.0, A.mult, -2048.0, A.add)
    tt(V("xe"), V("xc"), V("xb"), A.add)
    cp(X("lp", rank, sl(80, 94)), V("mus", 0, 14))
    tt(X("lp", rank, sl(0, 80)), V("xd"), V("xe"), A.add)
    mask = topo.mask(core, cores[others[0]])
    total["sent"] = bits(mask)
    spread = RemoteDMATransfer(dst_ids=[DstId(rid=a[0], pnc=a[1]) for a in (topo.addr(cores[q]) for q in others)], dma_engine_mask=mask,
                               remote_sem=T.sem["a_lp"], srcs=[X("lp", rank)[0]], dsts=[X("lp", rank)[0] for _ in others])
    k0 = note("g", lambda: g.remote_dma_fused([spread], local_sem=T.sem["sent"]), 1500, [X("lp", rank)], [], token=("sent", total["sent"]))
    lands("a_lp", [(X("lp", q), q) for q in others], [k0], 100)
    for j in others + [rank]:
        cp(X("s16", j), X("s32", j))
    ks = [send(j, D("dr", PLACE[rank]), X("s16", j), "a_r") for j in others]
    for k in ks:
        calls[k]["after"].add(k0)
    lands("a_r", [(D("dr", PLACE[q]), q) for q in others], ks, 240)
    dmas("l_dr", [("s", D("dr", PLACE[rank]), X("s16", rank))], 80)
    dmas("l_r", [("s", V("r16"), D("dr", sl(None)))], 320)
    ko = [hop("h_c%d" % j, X("so", j)) for j in others[1:]] + [send(others[0], D("dc", PLACE[rank]), X("so", others[0]), "a_c")]
    for k in ko:
        calls[k]["after"].update(ks)
    lands("a_c", [(D("dc", PLACE[q]), q) for q in others], ko, 256, 2)
    k1 = dmas("l_oc", [("s", V("ocs"), D("dc", sl(None)))], 512)
    note("g", lambda: g.affine_select(V("zq")[0], V("ones")[0], [[1, 516]], A.is_equal, 0.0, -4, -4), 1000, [V("ones")], [V("zq")], after=ko)
    dmas("l_ss", [("s", X("ss", j), T.stake[rows(j), :]) for j in others], 384, [k1])
    dmas("l_ds", [("s", D("ds", PLACE[rank]), T.stake[rows(rank), :])], 128, [k1])

    def EZ(i):
        return V("ez", 15 - i, 143 - i)

    def AM(s, t):
        return X("am", 0 if s == t else 1 + s * (s - 1) // 2 + t)

    def factors(s, on):
        for t in range(s - 1, -1, -1):
            if on == "v":
                ts(AM(s, t), AM(s, t + 1), mu(t), A.mult)
            else:
                act(AM(s, t), AM(s, t + 1), scale=mu(t))

    def candidates(w, k0, table, ps):
        cp(V("lc", 0, 16 * w), IND(V(table), V("gl", 0, w)))
        mms([(V(ps, 0, w), V("ib"), V("oa", 0, w), True, False)]
            + [(V(ps, 0, w), EZ(i), V("lc", i, 16 * w, 16), False, i == 15) for i in range(16)])
        nk = w // 16
        own_ = X("bb", sl(k0, k0 + nk) if nk > 1 else k0, sl(0, 16))
        ts(V("co", 0, w), V(ps, 0, w), 2048.0, A.add)
        ts(V("a8", 0, w), V("co", 0, w), 4088, A.bitwise_and)
        tt(own_, V("a8", 0, w), V("ptab", 0, w), A.is_equal)
        ts(V("xf", 0, w), own_, float(FAR), A.mult)
        tt(V("xg", 0, w), V("xf", 0, w), V("co", 0, w), A.max)
        cp(V("cl", k0 * 16, k0 * 16 + w), V("xg", 0, w))
        cp(V("cb", (k0 + 1) * 16, (k0 + 1) * 16 + w), V("a8", 0, w))

    def tables(s):
        act(V("tc", s, CW, S), one, scale=mu(7 + s))
        act(V("epw", s, CW, S), one, scale=mu(16 + s), bias=EPS)

    def preload(i, c):
        mms([(V(DB[c]), V("ib"), V("ones", 0, CW), True, False)])
        act(V(DB[c]), V("og") if c in SCAN[i] else X("do", chunk(c)))

    mms([(V(CUR, 0, 96), V("sel", 96 - 32 * PLACE[q], 224 - 32 * PLACE[q]), X("lp", q), k == 0, k == N - 1) for k, q in enumerate([rank] + others)])
    cp(V("lh", 0, 80), V(CUR, 0, 80))
    ts(V("xo"), V(CUR, 0, 80), 2048.0, A.add)
    ts(V("muf", 0, 14), V(CUR, 80, 94), 0.5, A.mult)
    ts(V("muf", 16, 23), V(CUR, 87, 94), -EPS / 2, A.mult)
    ts(V("muf", 24, 31), V(CUR, 87, 94), 0.25, A.mult)
    for b in range(3):
        blocks = range(6 * b, min(6 * b + 6, 16))
        mms([(V(DIST[b], 80 * (i - 6 * b), 80 * (i - 6 * b + 1)), X("bi", i), V("lh", 0, 80), True, True) for i in blocks])
        (cp if b == 1 else act)(V("lrep", 8 + 480 * b, 8 + 480 * b + 80 * len(blocks)), V(DIST[b], 0, 80 * len(blocks)))
    ts(V("xa"), V("xo"), 3, A.arith_shift_right, 15, A.bitwise_and)
    ts(V("xb"), V("xo"), 7, A.arith_shift_right, 15, A.bitwise_and)
    ts(V("xc"), V("xo"), 7, A.bitwise_and)
    ts(V("hm"), V("lh", 0, 80), 0.0, A.is_lt)
    ts(V("xd"), V("xa"), 80.0, A.mult, 8.0, A.add)
    ts(V("xe"), V("xc"), 16.0, A.mult)
    tt(V("xf"), V("xd"), V("xb"), A.add)
    tt(V("xg"), V("xf"), V("xe"), A.add)
    tt(V("xh"), V("xg"), V("hm"), A.mult)
    cp(V("gl"), V("xh"))
    ts(V("oa"), V("lh", 0, 80), 0.0, A.max)
    ts(V("a0"), V("xo", 0, 16), 4088, A.bitwise_and)
    cp(V("cb", 0, 16), V("a0"))
    cp(V("ln", 0, 80), V("xo"))
    candidates(80, 0, "lrep", DIST[2])
    for s in range(F0 + 1):
        factors(s, "a")
    for s in range(F0):
        tables(s)

    for b in range(3):
        mms([(V(DB[b], 0, min(512, 1280 - 512 * b)), V("rot16"), V("r16", 512 * b, min(512 * b + 512, 1280)), True, True)])
    act(X("rc", F0 - 1), slot("r16", F0 - 1), bias=M)
    act(X("rc", sl(0, 2)), slot("r16", 0, 2), bias=M)
    act(X("rc", sl(2, 4)), slot("r16", 2, 4), bias=M)
    for s in range(F0):
        ts(W(0, along(s)), slot("r16", s), M, A.add)
        away = W(0, along(s, P, 2 * P)), V(DB[s // 2], (s % 2) * P, (s % 2 + 1) * P)
        if s < F0 - 1:
            act(away[0], away[1], bias=M)
        else:
            ts(away[0], away[1], M, A.add)
    ts(V("muf", 32, 32 + F0), V("muf", 24, 24 + F0), K0 - 0.5, A.add)
    fill(V("muf", 32 + F0, 40), K0 - 0.5)
    tt(V("muf", 41, 48), V("muf", 0, 7), V("muf", 32, 39), A.mult)
    tt(V("muf", 49, 56), V("muf", 33, 40), V("muf", 41, 48), A.subtract)
    for s in range(S):
        act(V("ta", s, CW, S), one, scale=mu(s - 1) if s else 0.0)
        act(X("d3", along(s)), slot("ocs", s), scale=0.0625, bias=mu(48 + s if s else 32))
    for c in range(NC):
        scan(X("do", chunk(c)), V("ta"), X("d3", chunk(c)))

    def newest(r, view, bias):
        act(X("mer", r), view, bias=bias)
        k = send(others[-1], X("mn", r), X("mer", r), "a_mn%d" % r)
        lands("a_mn%d" % r, [(X("mn", r), others[0])], [k], 128)
        return k
    k0 = newest(0, slot("r16", F0 - 1), 0.0)
    ks = [hop("h_s%d" % j, X("ss", j)) for j in others]
    for k in ks:
        calls[k]["after"].add(k0)
    lands("a_s", [(D("ds", PLACE[q]), q) for q in others], ks, 3000, 2)
    dmas("l_st", [("s", V("sts"), D("ds", sl(None)))], 512)

    def gathers(i, n, slots):
        for s in slots:
            tt(slot("tq", s), IND(win(i), V("ln", 16 * s, 16 * s + 16)), V("rn") if i % 2 == 0 and s == n - 1 else own(i, s), A.subtract)
            ts(slot("cq", s), slot("tq", s), 256.0, A.min, -256.0, A.max)
            for c in range(NC):
                z, d = V("cq", s * P + c * CS, s * P + (c + 1) * CS), V(DB[c], s, CW, S)
                if c in SCAN[i]:
                    items = [(d, AM(s, s), z, False, s == n - 1)]
                elif c and n in WIDE:
                    d = V(DB[c])
                    items = ([(V(DB[c], u, CW, S), AM(u, s), z, False, False) for u in range(s, n)]
                             + ([(d, V("ib"), V("big"), False, False), (d, V("nb"), V("big"), False, False), (d, V("ib"), V("epw"), False, True)] if s == n - 1 else []))
                else:
                    items = ([(V(DB[c], u, CW, S), AM(u, s), z, False, False) for u in range(s, n)]
                             + [(d, V("ib"), V("big", 0, CS), False, False), (d, V("nb"), V("big", 0, CS), False, False),
                                (d, V("ib"), V("epw", s, CW, S), False, s == n - 1)])
                for a in range(0, len(items), BATCH):
                    mms(items[a:a + BATCH])
                    if s or a:
                        calls[-1]["after"].add(closing[c])
                    else:
                        opening[c] = len(calls) - 1
                    closing[c] = len(calls) - 1
            if s == n - 1:
                turn = sorted(range(NC), key=lambda c: c not in SCAN[i])
                for c, e in zip(turn, turn[1:]):
                    in_turn([closing[c], opening[e]])
    closing, opening = {}, {}

    def result(i, h):
        half = sl(h * 128, (h + 1) * 128)
        for s in range(S):
            act(X("rc", s, half), W(i, along(s, h * 128, (h + 1) * 128)), bias=-M)
        for k in range(2):
            dmas("d_yr%d" % (2 * k + h), [("s", D("dyr", sl(2 * k + h, 4 * N, 4)), X("rc", sl(4 * k, 4 * k + 4), half))], 256)
            ks = []
            for q in others:
                piece = D("dyr", 4 * PLACE[q] + 2 * k + h)
                if (k, h) in RELAYED:
                    ks.append(hop("h_y%d" % (4 * q + 2 * k + h), piece))
                else:
                    ks.append(send(q, X("lyr", 2 * rank + k, half), piece, "a_yr%d" % (4 * rank + 2 * k + h)))
            for q in others:
                lands("a_yr%d" % (4 * q + 2 * k + h), [(X("lyr", 2 * q + k, half), q)], ks, 192, 1 + ((k, h) in RELAYED))

    def updates(i, n):
        last = i == 2 * RO - 1
        named = min(n if i % 2 else n - 1, S - 1)
        line = []
        for c in range(NC):
            x = XB[c % 2]
            if c in SCAN[i]:
                scan(V("d1", 0, CW), V("ta"), V(DB[c]))
                act(V("d1", CW, 2 * CW), V("d1", 0, CW), bias=M16)
                act(V(DB[c]), V("d1", CW, 2 * CW), bias=-M16)
            scan(V(x, 0, CW, -1), V("tc", 0, CW, -1), V(DB[c], 0, CW, -1))
            line.append(len(calls) - 1)
            if c in SCAN[i]:
                act(V(x), V(x), bias=EPS - 0.5)
            halves = [(0, CW)] if c < NC - 1 else [(0, P), (P, CW)]
            for h, (a, b) in enumerate(halves):
                here, there = sl(c * CW + a, c * CW + b), sl(P * S + c * CW + a, P * S + c * CW + b)
                tt(W(i + 1, here), W(i, here), V(x, a, b), A.add)
                line.append(len(calls) - 1)
                if not last:
                    (move if c == NC - 1 else act)(X("ow", here), W(i + 1, here))
                if AWAY[c] == "d":
                    dmas("w%d_%d" % (i, c), [("s", W(i + 1, there, rows(u, k)), W(i + 1, here, rows(v, k))) for u, v, k in moves], 400)
                elif AWAY[c] == "c":
                    for u, v, k in moves:
                        move(W(i + 1, there, rows(u, k)), W(i + 1, here, rows(v, k)))
                elif c < NC - 1:
                    mms([(V(DB[c], s, CW, S), V("rot"), W(i + 1, along(s, c * CS, (c + 1) * CS)), True, True) for s in range(named)])
                    move(W(i + 1, there), V(DB[c]))
                else:
                    mms([(V(TURN[h], 0, P), V("rot"), W(i + 1, here), True, True)])
                    move(W(i + 1, there), V(TURN[h], 0, P))
            if last and c % 2:
                result(i + 1, c // 2)
        in_turn(line)

    for r in range(RO):
        f = F0 + r
        n = f + 1
        i = 2 * r
        m = FIRST[f]

        def dist(k):
            k -= k >= m
            return V(DIST[k // 2], (k % 2) * P, (k % 2 + 1) * P)

        def first_of(k):
            return k * (k - 1) // 2 if k < m else m * (m - 1) // 2 + (k - m) * (k - m - 1) // 2

        def follow(k):
            w, a = 16 * (k + 1), 128 * k
            if k:
                lo, c1 = P * first_of(k), 128 + 96 * (k % 2)
                mms([(V(CUR, c1, c1 + 16 * k), EZ(u), V("lt", lo + u, lo + P * k, 16), u == 0, u == 15) for u in range(16)])
                ts(X("bb", k, sl(16, w)), V(CUR, c1, c1 + 16 * k), 8.5 / 16, A.is_lt)
                tt(V("pp", a, a + w), V(CUR, 0, w), X("bb", k, sl(0, w)), A.mult)
            else:
                cp(V("pp", a, a + w), X("bb", k, sl(0, w)))
            mms([(V(CUR, 0, w + 16), V("ib"), V("pp", a, a + w + 16), True, False)]
                + [(V(CUR, w, w + 16), V("nb"), V("pp", a + 16 * u, a + 16 * u + 16), False, u == k) for u in range(k + 1)])

        def choose(out, table, k, x):
            tt(X("pr", x, sl(0, 16 * k)), V(CUR, 0, 16 * k), table, A.mult)
            mms([(out, V("ib"), X("pr", x, sl(16 * u, 16 * u + 16)), u == 0, u == k - 1) for u in range(k)])

        for c in range(NC):
            preload(i, c)
        for k in range(f):
            tt(slot("td", k), IND(win(i), V("cl", k * 16, (k + 1) * 16)), own(i, f - 1), A.subtract)
            if k != m - 1:
                act(dist(k), slot("td", k), AF.Abs)
            if (k > 0 or m < f) and k != m:
                act(slot("xs", k), slot("td", k), AF.Abs)
        for k in range(f):
            for j in range(0 if k < m else m, k):
                tt(slot("lt", first_of(k) + j - m * (k >= m)), slot("xs", k), dist(j), A.is_lt)
        gathers(i, n, range(f))
        for k in range(m):
            follow(k)
        best, place = V(CUR, 320, 336), V(CUR, 336, 352)
        if m < f:
            choose(place, V("ix", 0, 16 * (m + 1)), m + 1, 0)
            choose(best, V("cb", 0, 16 * (m + 1)), m + 1, 1)
            ts(V("gi"), place, 0.0, A.add)
            cp(V("da"), IND(V("xs"), V("gi")))
            a0, a1, a2 = (V("cb", 16 * (k + 1), 16 * (k + 2)) for k in range(m, f))
            lo = P * first_of(m)
            mms([(V(CUR, 352, 400), EZ(u), V("lt", lo + u, lo + 3 * P, 16), u == 0, u == 15) for u in range(16)])
            ts(X("hw", 0), V(CUR, 352, 368), 8.5 / 16, A.is_lt, -1.0, A.mult)
            ts(X("hw", sl(1, 3)), V(CUR, 368, 400), 8.5 / 16, A.is_lt)
            tt(X("hw", 3), a2, a1, A.subtract)
            tt(X("hw", 4), a0, a2, A.subtract)
            tt(X("hz", 1, sl(1, 64, 4)), X("hw", 2), X("hw", 3), A.mult)
            tt(X("hw", 5), X("hw", 1), X("hw", 4), A.mult)
            tt(X("hw", 6), X("hw", 5), X("hz", 1, sl(1, 64, 4)), A.add)
            tt(X("hz", 1, sl(2, 64, 4)), X("hw", 0), X("hw", 6), A.mult)
            tt(X("hw", 7), a2, X("hz", 1, sl(1, 64, 4)), A.subtract)
            tt(X("hz", 1, sl(3, 64, 4)), X("hw", 7), X("hz", 1, sl(2, 64, 4)), A.subtract)
            tt(X("hz", 1, sl(0, 64, 4)), best, a2, A.subtract)
            for k in range(m, f):
                tt(X("l4", sl(f - k, 64, 4)), V("da"), dist(k), A.is_gt)
            mms([(V(CUR, 400, 464), EZ(u), X("l4", sl(None), u), u == 0, u == 15) for u in range(16)])
            ts(X("hz", 0), V(CUR, 400, 464), 8.5 / 16, A.is_lt)
            scan(X("hz", 2), X("hz", 0), X("hz", 1))
            best = X("hz", 2, sl(3, 64, 4))
        else:
            choose(best, V("cb", 0, 16 * (f + 1)), f + 1, 2)
        half = V(DIST[2 * (m == f)], 0, P)
        mms([(half, V("sh"), X("mer", r), True, False), (half, V("sh2"), X("mn", r), False, False), (half, V("ib"), V("qrt"), False, True)])
        act(V("rn"), half, bias=M)
        ts(V("ln", 16 * f, 16 * f + 16), best, f - 1.0, A.add)
        ts(V("lh", 16 * f, 16 * f + 16), best, f - 1.0 - 2048, A.add)
        act(V("yo2", 16 * r, 16 * r + 16), best, scale=0.125, bias=float(P * (f - 1)))
        if r < RO - 1:
            ts(V("gl", 0, 16), best, 0.125, A.mult, float(P), A.min)
            ts(V("oa", 0, 16), V("lh", 16 * f, 16 * f + 16), 0.0, A.max)
        gathers(i, n, [f])
        act(W(i, along(f)), V("rn"))
        updates(i, n)

        if r == 0 and any(SCAN):
            c = max(max(x, default=0) for x in SCAN)
            ts(V("muf", 57, 64), V("muf", 0, 7), -K0, A.mult, K0, A.add)
            for s in range(S):
                act(V("og", s, CW, S), V("ocs", s * P + c * CS, s * P + (c + 1) * CS), scale=0.0625, bias=mu(56 + s) if s else K0)
        for c in range(NC):
            preload(i + 1, c)
        if r < RO - 1:
            mms([(V(CUR, u, P, 16), X("bi", u), V("lh", 16 * (f - 1), 16 * f), True, True) for u in range(16)])
            act(V("tb", 0, P), V(CUR, 0, P))
            candidates(16, f, "tb", CUR)
            factors(n, "a")
            act(X("do", along(f)), X("do", along(f)), bias=mu(24 + f))
        else:
            ts(V("yo1"), V("lh", 80, 128), 0.0, A.is_ge, 1792.0, A.mult)
            tt(V("yos"), V("yo1"), V("yo2"), A.add)
            dmas("d_yo", [("s", D("dyo", sl(None)), V("yos"))], 24)
            lands("a_yo", [(X("lyo", q), q) for q in others], [send(q, X("lyo", rank), D("dyo", PLACE[q]), "a_yo") for q in others], 100)
            dmas("out", [("s", T.yo[rows(q), :], X("lyo", q)) for q in others] + [("s", T.yo[rows(rank), :], X("yos", parts=rows(PLACE[rank])))], 24)
        gathers(i + 1, n, range(n))
        updates(i + 1, n)
        if r < RO - 1:
            tables(f)
            newest(r + 1, W(i + 2, along(f)), -M)

    dmas("out", [("s", T.yr[rows(rank), :], X("rc", parts=rows(PLACE[rank])))], 500)
    for k in range(2):
        for q in others:
            dmas("out", [("s", T.yr[rows(q), 1024 * k:1024 * (k + 1)], X("lyr", 2 * q + k))], 128)

    for k in range(4):
        for s in (2 * k, 2 * k + 1):
            tt(slot("d1", s), IND(win(2 * RO), V("ln", 16 * s, 16 * s + 16)), X("rc", s), A.subtract)
        act(V(DB[k]), slot("d1", 2 * k, 2 * k + 2), AF.Sigmoid, scale=-1.0 / 256, bias=M / 256, more=0 if k else 1300)
        if k:
            calls[-1]["after"].add(closing[0])
        closing[0] = len(calls) - 1
    for k in range(2):
        tt(slot("d3", 2 * k, 2 * k + 2), V(DB[k]), slot("sts", 2 * k, 2 * k + 2), A.mult)
        mms([(V(TURN[0], 0, P), V("i32"), slot("d3", s), s == 0, s == 3) for s in (2 * k, 2 * k + 1)])
    tt(slot("d3", 4, 6), V(DB[2]), slot("sts", 4, 6), A.mult)
    tt(V(CUR), V(DB[3]), slot("sts", 6, 8), A.mult)
    tt(slot("d3", 6), V(CUR, 0, P), slot("d3", 4), A.add)
    tt(V(XB[0], 0, P), V(CUR, P, 2 * P), slot("d3", 5), A.add)
    tt(slot("d3", 7), V(TURN[0], 0, P), slot("d3", 6), A.add)
    tt(V("ys"), V(XB[0], 0, P), slot("d3", 7), A.add)
    ks = []
    for k, q in enumerate(others):
        a = 128 * PLACE[q] + 4
        mms([(V(DB[k], 0, CS), V("zq", a - c, a + 128 - c), V("ys", c * CS, (c + 1) * CS), c == 0, c == 3) for c in range(4)])
        cp(X("sy", q), V(DB[k], 0, CS))
        ks.append(send(q, X("ly", rank), X("sy", q), "a_y%d" % rank))
    dmas("out", [("a", T.y[rows(rank), :], X("ys", parts=rows(PLACE[rank])))], 32)
    for k, q in zip(reversed(ks), others):
        lands("a_y%d" % q, [(X("ly", q), q)], [k], 32)
        dmas("out", [("a", T.y[rows(q), :], X("ly", q))], 32)
    issue(calls, Q, T)
